import numpy as np, ml_dtypes
CORES = [40,41,42,43,44,45,46,47]
N = 8
BF = ml_dtypes.bfloat16
def gentries(a):
    return np.ascontiguousarray(a.reshape(8, 16, -1).transpose(0, 2, 1)).reshape(8, -1)
def gtable(e):
    e = np.asarray(e); return np.ascontiguousarray(e.reshape(8, -1, 16).transpose(0, 2, 1)).reshape(128, -1).astype(np.int32)
S, n, M, CAP, DM = 3, 2048, 32, 192, 63
def lists(prev, ship, heads):
    a = [np.stack([gentries(x) for x in v]).astype(np.int64) for v in (prev, ship, heads)]
    return a[0].reshape(N, 8, S - 1, n), a[1].reshape(N, 8, S - 1, N, CAP), a[2].reshape(N, 8, S, M)
def before(pv, sh):
    r = np.arange(N).reshape(-1, 1, 1, 1); g = np.arange(8).reshape(1, -1, 1, 1); t = np.arange(S - 1).reshape(1, 1, -1, 1)
    x = np.maximum(pv - n, 0); q = x // CAP; e = sh[q, g, t, r, x % CAP]
    return np.where(pv < n, r * n + pv, np.where(e < 0, -1, q * n + e))
def counts(rng, w, swaps):
    A = np.zeros((N, N), np.int64); i = np.arange(N)
    for k in range(1, N): A[i, (i + k) % N] = w[k - 1]
    A[i, i] = n - np.add.reduce(A, axis=1)
    lim = np.where(np.eye(N, dtype=bool), n, CAP)
    for k in range(swaps):
        a, b = rng.permutation(N)[:2]; c, e = rng.permutation(N)[:2]
        m = int(min(A[a, e], A[b, c], lim[a, c] - A[a, c], lim[b, e] - A[b, e])); x = int(rng.integers(0, m // 3 + 1))
        A[a, c] += x; A[b, e] += x; A[a, e] -= x; A[b, c] -= x
    return A
def mixed(rng):
    return [[counts(rng, rng.integers(CAP // 4, 3 * CAP // 4, N - 1), 3 * N) for g in range(8)] for t in range(S - 1)]
def evens(rng):
    h = np.arange(M) * (n // M) + rng.integers(-(n // M // 3), n // M // 3 + 1, (N, 8, S, M)); h[..., 0] = 0
    return h
def uneven(rng):
    m = np.arange(M); b = rng.integers(0, M, (N, 8, S, 1))
    return np.where(m <= b, m, n - M + m)
def shop(rng, hd, ways, noise, turn=False):
    pv = np.zeros((N, 8, S - 1, n), np.int64); sh = np.full((N, 8, S - 1, N, CAP), -1, np.int64); ph = np.zeros((N, 8, S, n), np.int64); i = np.arange(n)
    for r in range(N):
        for g in range(8):
            for t in range(S):
                h = hd[r, g, t]; m = np.searchsorted(h, i, side="right") - 1; size = np.append(h, n)[1:] - h
                ph[r, g, t] = (2 * (i - h[m]) + 1) * 32768 // size[m]
    for t in range(S - 1):
        for g in range(8):
            A = ways[t][g]; num = [[] for r in range(N)]; key = [[] for r in range(N)]
            for q in range(N):
                o = rng.permutation(n); e = np.add.accumulate(A[q])
                for r in range(N):
                    u = o[e[r] - A[q, r]:e[r]]
                    if r == q: num[r].append(u)
                    else:
                        sh[q, g, t, r, :len(u)] = u; num[r].append(n + CAP * q + np.arange(len(u)))
                    key[r].append(ph[q, g, t, u])
            for r in range(N):
                a = np.concatenate(num[r]); k = np.concatenate(key[r]) + rng.integers(-noise, noise + 1, n)
                if turn: k = 65536 - k
                place = np.argsort(ph[r, g, t + 1] * n + rng.permutation(n))
                pv[r, g, t, place] = a[np.argsort(k)]
    return {"prev": np.stack([gtable(x.reshape(8, -1)) for x in pv]), "ship": np.stack([gtable(x.reshape(8, -1)) for x in sh]), "heads": np.stack([gtable(x.reshape(8, -1)) for x in hd])}
def times_of(rng):
    top = rng.integers(15, DM + 1, (N, 128, 1))
    return np.floor(rng.random((N, 128, S * n)) * (top + 1)).astype(BF)
def setup_inputs(rng):
    return {"dur": times_of(rng), **shop(rng, evens(rng), mixed(rng), 1500)}
def setup_inputs_full(rng):
    ways = [[counts(rng, [[CAP] * (N - 1), [0] * (N - 1), [CAP] + [0] * (N - 2), [1] * (N - 1)][(g + t) % 4], 0) for g in range(8)] for t in range(S - 1)]
    return {"dur": times_of(rng), **shop(rng, evens(rng), ways, 1500)}
def setup_inputs_machines(rng):
    hd = uneven(rng)
    return {"dur": rng.integers(DM - 15, DM + 1, (N, 128, S * n)).astype(np.float32).astype(BF), **shop(rng, hd, mixed(rng), 1 << 20)}
def setup_inputs_turned(rng):
    ways = mixed(rng)
    for t in range(S - 1):
        for g in range(0, 8, 2): ways[t][g] = counts(rng, [0] * (N - 1), 0)
    return {"dur": np.full((N, 128, S * n), DM, np.float32).astype(BF), **shop(rng, uneven(rng), ways, 0, turn=True)}
def setup_inputs_ties(rng):
    c = rng.integers(1, DM + 1, (N, 128, 1)); z = rng.integers(0, 4, (N, 128, S * n)) > 0; z[:, ::2] = True
    c[:, ::2] = 8
    return {"dur": np.where(z, c, 0).astype(np.float32).astype(BF), **shop(rng, evens(rng), mixed(rng), 1500)}
def setup_inputs_spread(rng):
    e = rng.integers(0, 7, (N, 1, S * n))
    return {"dur": np.floor(rng.random((N, 128, S * n)) * np.exp2(e)).astype(BF), **shop(rng, evens(rng), mixed(rng), 6000)}
def check_inputs(d):
    bad = []; v = d["dur"].astype(np.float32)
    if not (np.isfinite(v).all() and (v >= 0).all() and (v <= DM).all() and (v == np.floor(v)).all()): bad.append("durations")
    pv, sh, hd = lists(d["prev"], d["ship"], d["heads"])
    if (hd[..., 0] != 0).any() or (hd[..., 1:] <= hd[..., :-1]).any() or (hd[..., -1] >= n).any(): bad.append("heads")
    own = np.arange(N)
    if (sh < -1).any() or (sh >= n).any() or ((sh[..., 1:] >= 0) & (sh[..., :-1] < 0)).any() or (sh[own, :, :, own] != -1).any(): bad.append("ship")
    if (pv < 0).any() or (pv >= n + N * CAP).any(): bad.append("prev")
    if bad: return bad
    b = np.sort(before(pv, sh).transpose(1, 2, 0, 3).reshape(8, S - 1, N * n), axis=-1)
    if (b != np.arange(N * n)).any() or np.count_nonzero(sh >= 0) != np.count_nonzero(pv >= n): bad.append("jobs")
    return bad
def reference(dur, prev, ship, heads):
    pv, sh, hd = lists(prev, ship, heads); g = np.arange(8)
    b = before(pv, sh).transpose(2, 3, 0, 1)
    d = np.ascontiguousarray(dur.astype(np.float32).astype(np.int64).reshape(N, 8, 16, S, n).transpose(3, 4, 0, 1, 2))
    st = np.zeros((N, 8, S, n), bool); np.put_along_axis(st, hd, True, axis=-1)
    st = np.ascontiguousarray(st.transpose(2, 3, 0, 1))[..., None]
    C = np.zeros((S, n, N, 8, 16), np.int64)
    for t in range(S):
        R = np.zeros((n, N, 8, 16), np.int64) if t == 0 else C[t - 1].transpose(1, 0, 2, 3).reshape(N * n, 8, 16)[b[t - 1], g]
        m = np.zeros((N, 8, 16), np.int64)
        for i in range(n):
            m = np.maximum(np.where(st[t, i], 0, m), R[i]) + d[t, i]; C[t, i] = m
    D = np.max(C[S - 1], axis=(0, 1))
    sl = np.zeros((S - 1, n, N, 8, 16), np.int64); B = np.zeros((n, N, 8, 16), np.int64)
    for t in range(S - 1, -1, -1):
        if t == S - 1: Q = np.broadcast_to(D, (n, N, 8, 16))
        else:
            w = np.zeros((N * n, 8, 16), np.int64); w[b[t], g] = B; Q = w.reshape(N, n, 8, 16).transpose(1, 0, 2, 3)
        B = np.zeros((n, N, 8, 16), np.int64); m = np.broadcast_to(D, (N, 8, 16))
        for i in range(n - 1, -1, -1):
            F = np.minimum(m, Q[i])
            if t < S - 1: sl[t, i] = F - C[t, i]
            B[i] = F - d[t, i]; m = np.where(st[t, i], D, B[i])
    y = sl.transpose(2, 3, 4, 0, 1).reshape(N, 128, (S - 1) * n)
    return {"y": y.astype(np.float32)}

@@ -1,0 +1,327 @@
+from concourse.bass import DstId, RemoteDMATransfer
+from concourse.mybir import AluOpType as A, AxisListType, ActivationFunctionType as AF
+
+n, CAP, NR = 2048, 192, 8
+SL = NR * CAP
+W = n + SL
+BIG = float(1 << 20)
+FAR = 8192.0
+OFF = 512
+ZW = 3712
+CFG = {"q1": [(1536, 2048, "s"), (1024, 1536, "s"), (512, 1024, "s"), (192, 512, "s"), (0, 192, "s")], "vsend": 3, "shipa": 4,
+       "fin": [(1408, 2048), (832, 1408), (320, 832), (0, 320)], "dpos": 0, "s2a": 3, "vact": 1}
+
+f32, bf, i32, u16 = "float32", "bfloat16", "int32", "uint16"
+SCRATCH = {k: ("sbuf", [128, c], d) for k, c, d in [
+    ("pv", 256, i32), ("sh", 192, i32), ("hd", 8, i32), ("hu", 8, u16),
+    ("d0", n, bf), ("d2", n, bf), ("a1", n, bf), ("b1", n, bf), ("m0", n + 16, bf), ("m2", n + 16, bf),
+    ("zer", 32, bf), ("neg", 32, bf), ("far", 224, f32), ("j16", 128, f32), ("pi", 4, i32), ("pm", 4, i32), ("pf", 4, f32),
+    ("idw", 128, f32), ("val", W, f32), ("z1", W, f32), ("z2", ZW, f32), ("z3", ZW, f32),
+    ("z1w", 224, f32), ("z2w", 128, f32), ("z3w", 128, f32),
+    ("ty", 192, i32), ("tu", 192, i32), ("tz", 192, f32), ("tw", 192, f32), ("py", 128, i32), ("pz", 128, f32), ("pw", 128, f32),
+    ("pu", 256, u16), ("su", 96, u16), ("so", 192, u16), ("po", 128, u16), ("l1", 128, u16), ("l0", 128, u16), ("ls", 96, u16),
+    ("f1", W, f32), ("w2", W + SL, f32), ("f0", W, f32), ("u2", n, f32), ("r1", n, f32), ("q1", n, f32),
+    ("p1", n, f32), ("x0", n, f32), ("mx", n, f32), ("sb1", SL, f32), ("sb3", SL, f32),
+    ("dh", 32, f32), ("fx", 32, f32), ("dall", 12, f32), ("dd", 4, f32)]}
+SCRATCH["s1"] = ("psum", [128, n], f32)
+SEMAPHORES = ["e%d" % k for k in range(130)] + ["arr1", "arr2", "arr3", "arrd", "sent"]
+
+
+def engine_sets(topo, src, peers):
+    eng = topo.engines(src, peers[0])
+    far = [p for p in peers if topo.die(p) != topo.die(src)]
+    near = [p for p in peers if topo.die(p) == topo.die(src)]
+    res = {}
+    for group, pool in ((far, eng[0::2]), (near, eng[1::2])):
+        size = {p: 1 for p in group}
+        grown = True
+        while grown:
+            grown = False
+            for p in sorted(group, key=lambda x: size[x]):
+                if sum(size.values()) + size[p] <= len(pool):
+                    size[p] *= 2
+                    grown = True
+                    break
+        at = 0
+        for p in group:
+            res[p] = pool[at:at + size[p]]
+            at += size[p]
+    return res
+
+
+def runs(slots):
+    out = []
+    for s in slots:
+        if out and out[-1][1] == s:
+            out[-1][1] = s + 1
+        else:
+            out.append([s, s + 1])
+    return out
+
+
+def rank_program(g, core, T, topo):
+    r = T.rank_of(core)
+    if r is None:
+        return
+    cores = list(T.cores)
+    others = [p for p in range(NR) if p != r]
+    mine = engine_sets(topo, core, [cores[p] for p in others])
+    coming = sum(len(engine_sets(topo, cores[p], [c for c in cores if c != cores[p]])[core]) for p in others)
+    V, S, Y = g.vector, g.scalar, g.sync
+    Q = {"v": V, "s": S, "y": Y, "g": g}
+    ops = []
+
+    def op(q, fn, rd, wr, dma=False, sem=None):
+        ops.append({"q": q, "fn": fn, "rd": rd, "wr": wr, "inc": 16 if dma else 1, "sem": sem})
+
+    def arrival(name, wr):
+        op("x", None, [], wr, sem=name)
+
+    def send(src, dst, sem, rd):
+        def fn():
+            tr = []
+            for p in others:
+                rid, pid, _ = topo.addr(cores[p])
+                tr.append(RemoteDMATransfer(dst_ids=[DstId(rid=rid, pnc=pid)], dma_engine_mask=sum(1 << e for e in mine[cores[p]]),
+                                            remote_sem=T.sem[sem], src=src(p), dst=dst(p)))
+            g.remote_dma_fused(tr, local_sem=T.sem.sent)
+            return None
+        op("g", fn, rd, [])
+
+    def ts(out, a, s1, s2, o0, o1, rd, wr):
+        if o1 is None:
+            op("v", lambda: V.tensor_scalar(out, a, s1, None, o0), rd, wr)
+        else:
+            op("v", lambda: V.tensor_scalar(out, a, s1, s2, o0, o1), rd, wr)
+
+    def tt(out, a, b, o, rd, wr):
+        op("v", lambda: V.tensor_tensor(out, a, b, o), rd, wr)
+
+    def cp(out, a, rd, wr):
+        op("v", lambda: V.tensor_copy(out, a), rd, wr)
+
+    def scan(out, d0, d1, init, o0, o1, rd, wr):
+        op("v", lambda: V.tensor_tensor_scan(out, d0, d1, init, o0, o1), rd, wr)
+
+    def act(out, a, func, rd, wr, **kw):
+        op("s", lambda: S.activation(out, a, func, **kw), rd, wr)
+
+    def dma(q, out, a, rd, wr):
+        op(q, lambda: Q[q].dma_start(out, a), rd, wr, dma=True)
+
+    def fill(name, lo, hi, c):
+        op("v", lambda: V.memset(T[name][:, lo:hi], c), [], [(name, lo, hi)])
+
+    def iota(name, lo, hi, step, base, mult, flt=True):
+        if flt:
+            op("g", lambda: g.iota(T[name][:, lo:hi], [[step, hi - lo]], base, mult, allow_small_or_imprecise_dtypes=True), [], [(name, lo, hi)])
+        else:
+            op("g", lambda: g.iota(T[name][:, lo:hi], [[step, hi - lo]], base, mult), [], [(name, lo, hi)])
+
+    def rev(name, lo, hi):
+        return T[name][:, hi - 1::-1] if lo == 0 else T[name][:, hi - 1:lo - 1:-1]
+
+    def whole(name):
+        return (name, 0, SCRATCH[name][1][1])
+
+    def gather(q, out, olo, win, wlo, whi, off, clo, chi):
+        src = T[win][:, wlo:whi].indirect(T[off][:, clo:chi])
+        ohi = olo + 16 * (chi - clo)
+        if q == "v":
+            cp(T[out][:, olo:ohi], src, [(win, wlo, whi), (off, clo, chi)], [(out, olo, ohi)])
+        else:
+            act(T[out][:, olo:ohi], src, AF.Copy, [(win, wlo, whi), (off, clo, chi)], [(out, olo, ohi)])
+
+    def ship_places(lo):
+        hi = lo + 96
+        a = lambda name: T[name][:, lo:hi]
+        return [
+            lambda: ts(a("ty"), a("sh"), 15, None, A.bitwise_and, None, [("sh", lo, hi)], [("ty", lo, hi)]),
+            lambda: ts(a("tu"), a("sh"), 65535, None, A.bitwise_and, None, [("sh", lo, hi)], [("tu", lo, hi)]),
+            lambda: ts(a("tz"), a("ty"), 2047.0, None, A.mult, None, [("ty", lo, hi)], [("tz", lo, hi)]),
+            lambda: tt(a("tw"), a("tu"), a("tz"), A.add, [("tu", lo, hi), ("tz", lo, hi)], [("tw", lo, hi)]),
+            lambda: tt(a("tz"), a("tw"), T.j16[:, 0:96], A.min, [("tw", lo, hi), ("j16", 0, 96)], [("tz", lo, hi)]),
+            lambda: ts(a("so"), a("tz"), 0.0625, None, A.mult, None, [("tz", lo, hi)], [("so", lo, hi)])]
+
+    def ship_inverse(z, lo, slots):
+        for a, b in runs(slots):
+            act(T[z][:, 0:ZW].indirect(T.so[:, lo + 12 * a:lo + 12 * b]), T.val[:, CAP * a:CAP * b], AF.Silu,
+                [("so", lo + 12 * a, lo + 12 * b), ("val", CAP * a, CAP * b)], [whole(z)])
+
+    dma("s", T.sh[:, :], T.ship[:, :], [], [whole("sh")])
+    dma("s", T.hd[:, 0:6], T.heads[:, :], [], [whole("hd")])
+    dma("y", T.pv[:, :], T.prev[:, :], [], [whole("pv")])
+    iota("val", 0, 512, 1, OFF, 0)
+    iota("j16", 0, 128, 256, 16 * n, 16)
+    iota("pi", 0, 1, 0, 0, 1, flt=False)
+    iota("val", 1024, SL, 1, OFF + 1024, 0)
+    iota("w2", W, W + SL, 0, 0, 0)
+    iota("val", SL, W, 1, OFF + SL, 0)
+    fill("far", 0, 224, FAR)
+    dma("y", T.z2[0:128:16, 0:n], T.far[:, 0:128], [whole("far")], [("z2", 0, n)])
+    dma("y", T.d0[:, :], T.dur[:, 0:n], [], [whole("d0")])
+    dma("y", T.d2[:, :], T.dur[:, 2 * n:3 * n], [], [whole("d2")])
+    dma("y", T.z1[0:128:16, :], T.far[:, :], [whole("far")], [whole("z1")])
+    dma("y", T.a1[:, :], T.dur[:, n:2 * n], [], [whole("a1")])
+    dma("y", T.b1[:, :], T.dur[:, n - 1:2 * n - 1], [], [whole("b1")])
+    dma("y", T.z3[0:128:16, 0:n], T.far[:, 0:128], [whole("far")], [("z3", 0, n)])
+    fill("zer", 0, 32, 0.0)
+    fill("neg", 0, 32, -BIG)
+    fill("dall", 0, 4, 0.0)
+    fill("m0", 0, n + 16, 1.0)
+    fill("m2", 0, n + 16, 1.0)
+    act(T.val[:, 512:1024], T.val[:, 0:512], AF.Silu, [("val", 0, 512)], [("val", 512, 1024)], bias=512.0)
+
+    sp = ship_places(96)
+    sp[0](); sp[1](); sp[2]()
+    cp(T.su[:, :], T.sh[:, 0:96], [("sh", 0, 96)], [whole("su")])
+    sp[3]()
+    cp(T.hu[:, 0:6], T.hd[:, 0:6], [whole("hd")], [whole("hu")])
+    sp[4]()
+    ts(T.py[:, :], T.pv[:, 0:128], 15, None, A.bitwise_and, None, [("pv", 0, 128)], [whole("py")])
+    sp[5]()
+    ship_inverse("z2", 96, others[:CFG["s2a"]])
+    cp(T.m0[:, 0:n].indirect(T.hu[:, 0:2]), T.zer[:, :], [whole("hu"), whole("zer")], [("m0", 0, n)])
+    ts(T.pz[:, :], T.py[:, :], 3583.0, None, A.mult, None, [whole("py")], [whole("pz")])
+    cp(T.m2[:, 0:n].indirect(T.hu[:, 4:6]), T.zer[:, :], [whole("hu"), whole("zer")], [("m2", 0, n)])
+    tt(T.pw[:, :], T.pv[:, 0:128], T.pz[:, :], A.add, [("pv", 0, 128), whole("pz")], [whole("pw")])
+    cp(T.pu[:, :], T.pv[:, :], [whole("pv")], [whole("pu")])
+    ts(T.po[:, :], T.pw[:, :], 0.0625, None, A.mult, None, [whole("pw")], [whole("po")])
+
+    scan(T.f1[:, 0:n], T.m0[:, 0:n], T.d0[:, :], 0.0, A.mult, A.add, [whole("m0"), whole("d0")], [("f1", 0, n)])
+    for a, b in runs(others):
+        gather("s", "sb1", CAP * a, "f1", 0, n, "su", 12 * a, 12 * b)
+    send(lambda p: T.sb1[:, CAP * p:CAP * p + CAP], lambda p: T.f1[:, n + CAP * r:n + CAP * r + CAP], "arr1", [whole("sb1")])
+    ship_inverse("z2", 96, others[CFG["s2a"]:])
+    dma("y", T.z2w[:, :], T.z2[0:128:16, 0:n], [("z2", 0, n)], [whole("z2w")])
+    act(T.z1[:, :].indirect(T.po[:, :]), T.val[:, SL:W], AF.Silu, [whole("po"), ("val", SL, W)], [whole("z1")])
+    dma("y", T.z1w[:, :], T.z1[0:128:16, :], [whole("z1")], [whole("z1w")])
+    scan(rev("u2", 0, n), rev("m2", 1, n + 1), rev("d2", 0, n), 0.0, A.mult, A.add, [whole("m2"), whole("d2")], [whole("u2")])
+    cp(T.w2[:, SL:SL + W].indirect(T.pu[:, 128:256]), T.u2[:, :], [("pu", 128, 256), whole("u2")], [("w2", SL, SL + W)])
+    send(lambda p: T.w2[:, W + CAP * p:W + CAP * p + CAP], lambda p: T.w2[:, CAP * r:CAP * r + CAP], "arr2", [("w2", W, W + SL)])
+    arrival("arr1", [("f1", n, W)])
+    arrival("arr2", [("w2", 0, SL)])
+
+    sp = ship_places(0)
+    sp[0](); sp[1]()
+    ts(T.pm[:, 0:1], T.pi[:, 0:1], 112, None, A.bitwise_and, None, [whole("pi")], [whole("pm")])
+    sp[2]()
+    ts(T.dh[:, :], T.a1[:, :].indirect(T.hu[:, 2:4]), BIG, None, A.add, None, [whole("a1"), whole("hu")], [whole("dh")])
+    sp[3]()
+    cp(T.pf[:, 0:1], T.pm[:, 0:1], [whole("pm")], [whole("pf")])
+    sp[4]()
+    cp(T.b1[:, :].indirect(T.hu[:, 2:4]), T.neg[:, :], [whole("hu"), whole("neg")], [whole("b1")])
+    sp[5]()
+    ts(T.idw[:, :], T.j16[:, :], 0.0625, T.pf[:, 0:1], A.mult, A.subtract, [whole("j16"), whole("pf")], [whole("idw")])
+    cp(T.a1[:, :].indirect(T.hu[:, 2:4]), T.neg[:, :], [whole("hu"), whole("neg")], [whole("a1")])
+    ship_inverse("z3", 0, others[:CFG["shipa"]])
+    if CFG["shipa"] == 7:
+        dma("y", T.z3w[:, :], T.z3[0:128:16, 0:n], [("z3", 0, n)], [whole("z3w")])
+    tt(T.idw[:, :], T.idw[:, :], T.z2w[:, :], A.min, [whole("idw"), whole("z2w")], [whole("idw")])
+    gather("v", "r1", 0, "f1", 0, W, "pu", 0, 128)
+    ts(T.l1[:, :], T.idw[:, :], 0.25 - OFF, None, A.add, None, [whole("idw")], [whole("l1")])
+    scan(T.s1[:, :], T.b1[:, :], T.r1[:, :], 0.0, A.add, A.max, [whole("b1"), whole("r1")], [whole("s1")])
+
+    ch = CFG["q1"]
+
+    def u1_scan(k):
+        lo, hi, _ = ch[k]
+        init = 0.0 if k == 0 else T.f0[:, SL + hi:SL + hi + 1]
+        scan(rev("f0", SL + lo, SL + hi), rev("q1", lo, hi), rev("a1", lo, hi), init, A.max, A.add,
+             [("q1", lo, hi), ("a1", lo, hi)] + ([] if k == 0 else [("f0", SL + hi, SL + hi + 1)]), [("f0", SL + lo, SL + hi)])
+    done = 0
+    for k, (lo, hi, q) in enumerate(ch):
+        gather(q, "q1", lo, "w2", 0, W, "l1", lo // 16, hi // 16)
+        if k == 0:
+            ts(T.ls[:, :], T.z1w[:, 128:224], 0.25 - n, n - 0.75, A.add, A.min, [whole("z1w")], [whole("ls")])
+        if q == "v" and k > 0:
+            while done < k:
+                u1_scan(done)
+                done += 1
+    while done < len(ch):
+        u1_scan(done)
+        done += 1
+    tt(T.fx[:, :], T.f0[:, SL:W].indirect(T.hu[:, 2:4]), T.dh[:, :], A.add, [("f0", SL, W), whole("hu"), whole("dh")], [whole("fx")])
+    cp(T.f0[:, SL:W].indirect(T.hu[:, 2:4]), T.fx[:, :], [whole("hu"), whole("fx")], [("f0", SL, W)])
+    for q, slots in (("s", others[CFG["vsend"]:]), ("v", others[:CFG["vsend"]])):
+        for a, b in runs(slots):
+            gather(q, "sb3", CAP * a, "f0", SL, W, "ls", 12 * a, 12 * b)
+    send(lambda p: T.sb3[:, CAP * p:CAP * p + CAP], lambda p: T.f0[:, CAP * r:CAP * r + CAP], "arr3", [whole("sb3")])
+    arrival("arr3", [("f0", 0, SL)])
+    if CFG["shipa"] < 7:
+        ship_inverse("z3", 0, others[CFG["shipa"]:])
+        dma("y", T.z3w[:, :], T.z3[0:128:16, 0:n], [("z3", 0, n)], [whole("z3w")])
+
+    tt(T.p1[:, :], T.f0[:, SL:W], T.s1[:, :], A.add, [("f0", SL, W), whole("s1")], [whole("p1")])
+    op("v", lambda: V.tensor_reduce(T.dall[:, 0:1], T.p1[:, :], AxisListType.X, A.max), [whole("p1")], [("dall", 0, 4)])
+    place = lambda p: 4 + (r if r < p else r - 1)
+    send(lambda p: T.dall[:, 0:1], lambda p: T.dall[:, place(p):place(p) + 1], "arrd", [("dall", 0, 4)])
+    arrival("arrd", [("dall", 4, 12)])
+    tt(T.z3w[:, :], T.z3w[:, :], T.z1w[:, 0:128], A.min, [whole("z3w"), whole("z1w")], [whole("z3w")])
+    ts(T.l0[:, :], T.z3w[:, :], 0.25 - OFF, None, A.add, None, [whole("z3w")], [whole("l0")])
+
+    fin = CFG["fin"]
+
+    def x_gather(k):
+        lo, hi = fin[k]
+        tt(T.x0[:, lo:hi], T.f0[:, :].indirect(T.l0[:, lo // 16:hi // 16]), T.f1[:, lo:hi], A.add,
+           [whole("f0"), whole("l0"), ("f1", lo, hi)], [("x0", lo, hi)])
+
+    def m_scan(k):
+        lo, hi = fin[k]
+        init = 0.0 if k == 0 else T.mx[:, hi:hi + 1]
+        scan(rev("mx", lo, hi), rev("m0", lo + 1, hi + 1), rev("x0", lo, hi), init, A.mult, A.max,
+             [whole("m0"), ("x0", lo, hi)] + ([] if k == 0 else [("mx", hi, hi + 1)]), [("mx", lo, hi)])
+
+    def slack(q, out, src, lo, hi, at):
+        if q == "s":
+            act(T[out][:, lo:hi], T[src][:, lo:hi], AF.Identity, [(src, lo, hi), whole("dd")], [(out, lo, hi)], bias=T.dd[:, 0:1], scale=-1.0)
+        else:
+            ts(T[out][:, lo:hi], T[src][:, lo:hi], -1.0, T.dd[:, 0:1], A.mult, A.add, [(src, lo, hi), whole("dd")], [(out, lo, hi)])
+        dma("y", T.y[:, at + lo:at + hi], T[out][:, lo:hi], [(out, lo, hi)], [("y", at + lo, at + hi)])
+
+    def end_of_plan():
+        op("v", lambda: V.tensor_reduce(T.dd[:, 0:1], T.dall[:, 0:11], AxisListType.X, A.max), [whole("dall")], [whole("dd")])
+    x_gather(0)
+    if CFG["dpos"] == 0:
+        end_of_plan()
+    halves = [(0, n // 2), (n // 2, n)]
+    for k in range(len(fin)):
+        if k + 1 < len(fin):
+            x_gather(k + 1)
+        m_scan(k)
+        if k + 1 == CFG["dpos"]:
+            end_of_plan()
+    for k in range(len(fin)):
+        if k < len(halves):
+            slack("s", "p1", "p1", halves[k][0], halves[k][1], n)
+        slack("s" if k + CFG["vact"] < len(fin) else "v", "x0", "mx", fin[k][0], fin[k][1], 0)
+    op("y", None, [("y", 0, 2 * n)], [])
+
+    def meet(a, b):
+        return any(x[0] == z[0] and x[1] < z[2] and z[1] < x[2] for x in a for z in b)
+    known = {q: set() for q in "vsygx"}
+    closure, waits, used = [], [], set()
+    for k, o in enumerate(ops):
+        deps = [j for j in range(k) if meet(ops[j]["wr"], o["rd"] + o["wr"]) or meet(ops[j]["rd"], o["wr"])]
+        if o["q"] == "x":
+            deps = []
+        kn, w = known[o["q"]], []
+        for j in sorted(deps, reverse=True):
+            if j not in kn:
+                w.append(j)
+                kn |= closure[j]
+        waits.append(w)
+        used |= set(w)
+        closure.append((set() if o["q"] == "x" else set(kn)) | {k})
+    sems = {}
+    for j in sorted(used):
+        sems[j] = (T.sem[ops[j]["sem"]], coming) if ops[j]["sem"] else (T.sem["e%d" % len(sems)], ops[j]["inc"])
+    for k, o in enumerate(ops):
+        for j in reversed(waits[k]):
+            Q[o["q"]].wait_ge(sems[j][0], sems[j][1])
+        if o["fn"] is not None:
+            ins = o["fn"]()
+            if k in sems:
+                ins.then_inc(sems[k][0], sems[k][1])
+    g.wait_ge(T.sem.sent, 4 * sum(len(e) for e in mine.values()))

@@ -8,22 +8,22 @@ BIG = float(1 << 20)
 FAR = 8192.0
 OFF = 512
 ZW = 3712
-CFG = {"q1": [(1536, 2048, "s"), (1024, 1536, "s"), (512, 1024, "s"), (192, 512, "s"), (0, 192, "s")], "vsend": 3, "shipa": 4,
-       "fin": [(1408, 2048), (832, 1408), (320, 832), (0, 320)], "dpos": 0, "s2a": 3, "vact": 1}
+CFG = {"q1": [(1536, 2048, "s"), (1024, 1536, "s"), (512, 1024, "s"), (0, 512, "s")], "vsend": 0, "shipa": 2, "s2a": 3,
+       "y1q": "sv", "l0e": 0, "vship": 0, "c1late": 1,
+       "fq": [(1664, 2048, "v"), (1152, 1664, "s"), (640, 1152, "s"), (256, 640, "s"), (0, 256, "s")], "st": [0, 1, 2, 3, 4]}
 
 f32, bf, i32, u16 = "float32", "bfloat16", "int32", "uint16"
 SCRATCH = {k: ("sbuf", [128, c], d) for k, c, d in [
     ("pv", 256, i32), ("sh", 192, i32), ("hd", 8, i32), ("hu", 8, u16),
-    ("d0", n, bf), ("d2", n, bf), ("a1", n, bf), ("b1", n, bf), ("m0", n + 16, bf), ("m2", n + 16, bf),
-    ("zer", 32, bf), ("neg", 32, bf), ("far", 224, f32), ("j16", 128, f32), ("pi", 4, i32), ("pm", 4, i32), ("pf", 4, f32),
+    ("d0", n, bf), ("d2", n, bf), ("a1", n + 16, bf), ("d1", n, bf), ("m0", n + 16, bf), ("m2", n + 16, bf),
+    ("zer", 32, bf), ("neg", 32, bf), ("pos", 32, bf), ("far", 224, f32), ("j16", 128, f32), ("pi", 4, i32), ("pm", 4, i32), ("pf", 4, f32),
     ("idw", 128, f32), ("val", W, f32), ("z1", W, f32), ("z2", ZW, f32), ("z3", ZW, f32),
     ("z1w", 224, f32), ("z2w", 128, f32), ("z3w", 128, f32),
     ("ty", 192, i32), ("tu", 192, i32), ("tz", 192, f32), ("tw", 192, f32), ("py", 128, i32), ("pz", 128, f32), ("pw", 128, f32),
     ("pu", 256, u16), ("su", 96, u16), ("so", 192, u16), ("po", 128, u16), ("l1", 128, u16), ("l0", 128, u16), ("ls", 96, u16),
-    ("f1", W, f32), ("w2", W + SL, f32), ("f0", W, f32), ("u2", n, f32), ("r1", n, f32), ("q1", n, f32),
-    ("p1", n, f32), ("x0", n, f32), ("mx", n, f32), ("sb1", SL, f32), ("sb3", SL, f32),
-    ("dh", 32, f32), ("fx", 32, f32), ("dall", 12, f32), ("dd", 4, f32)]}
-SCRATCH["s1"] = ("psum", [128, n], f32)
+    ("f1", W, f32), ("w2", W + SL, f32), ("f0", W, f32), ("u2", n, f32), ("r1", n, f32), ("q1", n, f32), ("c1", n, f32),
+    ("p1", n, f32), ("x0", n, f32), ("mx", n, f32), ("sb1", SL, f32), ("sb3", SL, f32), ("dall", 12, f32), ("dd", 4, f32)]}
+SCRATCH["t1"] = ("psum", [128, n], f32)
 SEMAPHORES = ["e%d" % k for k in range(130)] + ["arr1", "arr2", "arr3", "arrd", "sent"]
 
 
@@ -143,10 +143,13 @@ def rank_program(g, core, T, topo):
             lambda: tt(a("tz"), a("tw"), T.j16[:, 0:96], A.min, [("tw", lo, hi), ("j16", 0, 96)], [("tz", lo, hi)]),
             lambda: ts(a("so"), a("tz"), 0.0625, None, A.mult, None, [("tz", lo, hi)], [("so", lo, hi)])]
 
-    def ship_inverse(z, lo, slots):
+    def ship_inverse(z, lo, slots, q="s"):
         for a, b in runs(slots):
-            act(T[z][:, 0:ZW].indirect(T.so[:, lo + 12 * a:lo + 12 * b]), T.val[:, CAP * a:CAP * b], AF.Silu,
-                [("so", lo + 12 * a, lo + 12 * b), ("val", CAP * a, CAP * b)], [whole(z)])
+            out, rd = T[z][:, 0:ZW].indirect(T.so[:, lo + 12 * a:lo + 12 * b]), [("so", lo + 12 * a, lo + 12 * b), ("val", CAP * a, CAP * b)]
+            if q == "s":
+                act(out, T.val[:, CAP * a:CAP * b], AF.Silu, rd, [whole(z)])
+            else:
+                cp(out, T.val[:, CAP * a:CAP * b], rd, [whole(z)])
 
     dma("s", T.sh[:, :], T.ship[:, :], [], [whole("sh")])
     dma("s", T.hd[:, 0:6], T.heads[:, :], [], [whole("hd")])
@@ -155,22 +158,23 @@ def rank_program(g, core, T, topo):
     iota("j16", 0, 128, 256, 16 * n, 16)
     iota("pi", 0, 1, 0, 0, 1, flt=False)
     iota("val", 1024, SL, 1, OFF + 1024, 0)
-    iota("w2", W, W + SL, 0, 0, 0)
     iota("val", SL, W, 1, OFF + SL, 0)
     fill("far", 0, 224, FAR)
     dma("y", T.z2[0:128:16, 0:n], T.far[:, 0:128], [whole("far")], [("z2", 0, n)])
     dma("y", T.d0[:, :], T.dur[:, 0:n], [], [whole("d0")])
     dma("y", T.d2[:, :], T.dur[:, 2 * n:3 * n], [], [whole("d2")])
     dma("y", T.z1[0:128:16, :], T.far[:, :], [whole("far")], [whole("z1")])
-    dma("y", T.a1[:, :], T.dur[:, n:2 * n], [], [whole("a1")])
-    dma("y", T.b1[:, :], T.dur[:, n - 1:2 * n - 1], [], [whole("b1")])
-    dma("y", T.z3[0:128:16, 0:n], T.far[:, 0:128], [whole("far")], [("z3", 0, n)])
     fill("zer", 0, 32, 0.0)
     fill("neg", 0, 32, -BIG)
+    fill("pos", 0, 32, BIG)
     fill("dall", 0, 4, 0.0)
     fill("m0", 0, n + 16, 1.0)
     fill("m2", 0, n + 16, 1.0)
     act(T.val[:, 512:1024], T.val[:, 0:512], AF.Silu, [("val", 0, 512)], [("val", 512, 1024)], bias=512.0)
+    dma("y", T.w2[:, W:W + SL], T.val[:, 0:SL], [("val", 0, SL)], [("w2", W, W + SL)])
+    dma("y", T.a1[:, :], T.dur[:, n:2 * n + 16], [], [whole("a1")])
+    dma("y", T.d1[:, :], T.dur[:, n:2 * n], [], [whole("d1")])
+    dma("y", T.z3[0:128:16, 0:n], T.far[:, 0:128], [whole("far")], [("z3", 0, n)])
 
     sp = ship_places(96)
     sp[0](); sp[1](); sp[2]()
@@ -178,17 +182,17 @@ def rank_program(g, core, T, topo):
     sp[3]()
     cp(T.hu[:, 0:6], T.hd[:, 0:6], [whole("hd")], [whole("hu")])
     sp[4]()
-    ts(T.py[:, :], T.pv[:, 0:128], 15, None, A.bitwise_and, None, [("pv", 0, 128)], [whole("py")])
+    cp(T.m0[:, 0:n].indirect(T.hu[:, 0:2]), T.zer[:, :], [whole("hu"), whole("zer")], [("m0", 0, n)])
     sp[5]()
     ship_inverse("z2", 96, others[:CFG["s2a"]])
-    cp(T.m0[:, 0:n].indirect(T.hu[:, 0:2]), T.zer[:, :], [whole("hu"), whole("zer")], [("m0", 0, n)])
-    ts(T.pz[:, :], T.py[:, :], 3583.0, None, A.mult, None, [whole("py")], [whole("pz")])
     cp(T.m2[:, 0:n].indirect(T.hu[:, 4:6]), T.zer[:, :], [whole("hu"), whole("zer")], [("m2", 0, n)])
-    tt(T.pw[:, :], T.pv[:, 0:128], T.pz[:, :], A.add, [("pv", 0, 128), whole("pz")], [whole("pw")])
-    cp(T.pu[:, :], T.pv[:, :], [whole("pv")], [whole("pu")])
-    ts(T.po[:, :], T.pw[:, :], 0.0625, None, A.mult, None, [whole("pw")], [whole("po")])
-
+    ts(T.py[:, :], T.pv[:, 0:128], 15, None, A.bitwise_and, None, [("pv", 0, 128)], [whole("py")])
     scan(T.f1[:, 0:n], T.m0[:, 0:n], T.d0[:, :], 0.0, A.mult, A.add, [whole("m0"), whole("d0")], [("f1", 0, n)])
+    ts(T.pz[:, :], T.py[:, :], 3583.0, None, A.mult, None, [whole("py")], [whole("pz")])
+    cp(T.pu[:, :], T.pv[:, :], [whole("pv")], [whole("pu")])
+    tt(T.pw[:, :], T.pv[:, 0:128], T.pz[:, :], A.add, [("pv", 0, 128), whole("pz")], [whole("pw")])
+    scan(rev("u2", 0, n), rev("m2", 1, n + 1), rev("d2", 0, n), 0.0, A.mult, A.add, [whole("m2"), whole("d2")], [whole("u2")])
+    ts(T.po[:, :], T.pw[:, :], 0.0625, None, A.mult, None, [whole("pw")], [whole("po")])
     for a, b in runs(others):
         gather("s", "sb1", CAP * a, "f1", 0, n, "su", 12 * a, 12 * b)
     send(lambda p: T.sb1[:, CAP * p:CAP * p + CAP], lambda p: T.f1[:, n + CAP * r:n + CAP * r + CAP], "arr1", [whole("sb1")])
@@ -196,9 +200,9 @@ def rank_program(g, core, T, topo):
     dma("y", T.z2w[:, :], T.z2[0:128:16, 0:n], [("z2", 0, n)], [whole("z2w")])
     act(T.z1[:, :].indirect(T.po[:, :]), T.val[:, SL:W], AF.Silu, [whole("po"), ("val", SL, W)], [whole("z1")])
     dma("y", T.z1w[:, :], T.z1[0:128:16, :], [whole("z1")], [whole("z1w")])
-    scan(rev("u2", 0, n), rev("m2", 1, n + 1), rev("d2", 0, n), 0.0, A.mult, A.add, [whole("m2"), whole("d2")], [whole("u2")])
     cp(T.w2[:, SL:SL + W].indirect(T.pu[:, 128:256]), T.u2[:, :], [("pu", 128, 256), whole("u2")], [("w2", SL, SL + W)])
     send(lambda p: T.w2[:, W + CAP * p:W + CAP * p + CAP], lambda p: T.w2[:, CAP * r:CAP * r + CAP], "arr2", [("w2", W, W + SL)])
+    iota("m2", 0, n + 16, 0, 0, 0)
     arrival("arr1", [("f1", n, W)])
     arrival("arr2", [("w2", 0, SL)])
 
@@ -206,96 +210,91 @@ def rank_program(g, core, T, topo):
     sp[0](); sp[1]()
     ts(T.pm[:, 0:1], T.pi[:, 0:1], 112, None, A.bitwise_and, None, [whole("pi")], [whole("pm")])
     sp[2]()
-    ts(T.dh[:, :], T.a1[:, :].indirect(T.hu[:, 2:4]), BIG, None, A.add, None, [whole("a1"), whole("hu")], [whole("dh")])
-    sp[3]()
     cp(T.pf[:, 0:1], T.pm[:, 0:1], [whole("pm")], [whole("pf")])
-    sp[4]()
-    cp(T.b1[:, :].indirect(T.hu[:, 2:4]), T.neg[:, :], [whole("hu"), whole("neg")], [whole("b1")])
-    sp[5]()
+    sp[3]()
     ts(T.idw[:, :], T.j16[:, :], 0.0625, T.pf[:, 0:1], A.mult, A.subtract, [whole("j16"), whole("pf")], [whole("idw")])
-    cp(T.a1[:, :].indirect(T.hu[:, 2:4]), T.neg[:, :], [whole("hu"), whole("neg")], [whole("a1")])
-    ship_inverse("z3", 0, others[:CFG["shipa"]])
-    if CFG["shipa"] == 7:
-        dma("y", T.z3w[:, :], T.z3[0:128:16, 0:n], [("z3", 0, n)], [whole("z3w")])
+    sp[4]()
     tt(T.idw[:, :], T.idw[:, :], T.z2w[:, :], A.min, [whole("idw"), whole("z2w")], [whole("idw")])
-    gather("v", "r1", 0, "f1", 0, W, "pu", 0, 128)
+    sp[5]()
     ts(T.l1[:, :], T.idw[:, :], 0.25 - OFF, None, A.add, None, [whole("idw")], [whole("l1")])
-    scan(T.s1[:, :], T.b1[:, :], T.r1[:, :], 0.0, A.add, A.max, [whole("b1"), whole("r1")], [whole("s1")])
+    cp(T.a1[:, :].indirect(T.hu[:, 2:4]), T.neg[:, :], [whole("hu"), whole("neg")], [whole("a1")])
+    nv, na = CFG["vship"], CFG["vship"] + CFG["shipa"]
+    ship_inverse("z3", 0, others[:nv], "v")
+    ship_inverse("z3", 0, others[nv:na])
+    tt(T.r1[:, :], T.f1[:, :].indirect(T.pu[:, 0:128]), T.d1[:, :], A.add, [whole("f1"), ("pu", 0, 128), whole("d1")], [whole("r1")])
+
+    def c1_scan():
+        scan(T.c1[:, :], T.a1[:, 0:n], T.r1[:, :], 0.0, A.add, A.max, [whole("a1"), whole("r1")], [whole("c1")])
+    if not CFG["c1late"]:
+        c1_scan()
 
     ch = CFG["q1"]
 
-    def u1_scan(k):
+    def x1_add(k):
         lo, hi, _ = ch[k]
-        init = 0.0 if k == 0 else T.f0[:, SL + hi:SL + hi + 1]
-        scan(rev("f0", SL + lo, SL + hi), rev("q1", lo, hi), rev("a1", lo, hi), init, A.max, A.add,
-             [("q1", lo, hi), ("a1", lo, hi)] + ([] if k == 0 else [("f0", SL + hi, SL + hi + 1)]), [("f0", SL + lo, SL + hi)])
-    done = 0
+        tt(T.f0[:, SL + lo:SL + hi], T.r1[:, lo:hi], T.t1[:, lo:hi], A.add, [("r1", lo, hi), ("t1", lo, hi)], [("f0", SL + lo, SL + hi)])
     for k, (lo, hi, q) in enumerate(ch):
         gather(q, "q1", lo, "w2", 0, W, "l1", lo // 16, hi // 16)
-        if k == 0:
+    for k, (lo, hi, q) in enumerate(ch):
+        init = -BIG if k == 0 else T.t1[:, hi:hi + 1]
+        scan(rev("t1", lo, hi), rev("a1", lo + 1, hi + 1), rev("q1", lo, hi), init, A.add, A.max,
+             [("q1", lo, hi), whole("a1")] + ([] if k == 0 else [("t1", hi, hi + 1)]), [("t1", lo, hi)])
+        if k > 0:
+            x1_add(k - 1)
+        else:
             ts(T.ls[:, :], T.z1w[:, 128:224], 0.25 - n, n - 0.75, A.add, A.min, [whole("z1w")], [whole("ls")])
-        if q == "v" and k > 0:
-            while done < k:
-                u1_scan(done)
-                done += 1
-    while done < len(ch):
-        u1_scan(done)
-        done += 1
-    tt(T.fx[:, :], T.f0[:, SL:W].indirect(T.hu[:, 2:4]), T.dh[:, :], A.add, [("f0", SL, W), whole("hu"), whole("dh")], [whole("fx")])
-    cp(T.f0[:, SL:W].indirect(T.hu[:, 2:4]), T.fx[:, :], [whole("hu"), whole("fx")], [("f0", SL, W)])
+    x1_add(len(ch) - 1)
+    ship_inverse("z3", 0, others[na:])
+    dma("y", T.z3w[:, :], T.z3[0:128:16, 0:n], [("z3", 0, n)], [whole("z3w")])
     for q, slots in (("s", others[CFG["vsend"]:]), ("v", others[:CFG["vsend"]])):
         for a, b in runs(slots):
             gather(q, "sb3", CAP * a, "f0", SL, W, "ls", 12 * a, 12 * b)
-    send(lambda p: T.sb3[:, CAP * p:CAP * p + CAP], lambda p: T.f0[:, CAP * r:CAP * r + CAP], "arr3", [whole("sb3")])
-    arrival("arr3", [("f0", 0, SL)])
-    if CFG["shipa"] < 7:
-        ship_inverse("z3", 0, others[CFG["shipa"]:])
-        dma("y", T.z3w[:, :], T.z3[0:128:16, 0:n], [("z3", 0, n)], [whole("z3w")])
-
-    tt(T.p1[:, :], T.f0[:, SL:W], T.s1[:, :], A.add, [("f0", SL, W), whole("s1")], [whole("p1")])
-    op("v", lambda: V.tensor_reduce(T.dall[:, 0:1], T.p1[:, :], AxisListType.X, A.max), [whole("p1")], [("dall", 0, 4)])
+    op("v", lambda: V.tensor_reduce(T.dall[:, 0:1], T.f0[:, SL:W], AxisListType.X, A.max), [("f0", SL, W)], [("dall", 0, 4)])
     place = lambda p: 4 + (r if r < p else r - 1)
     send(lambda p: T.dall[:, 0:1], lambda p: T.dall[:, place(p):place(p) + 1], "arrd", [("dall", 0, 4)])
+    send(lambda p: T.sb3[:, CAP * p:CAP * p + CAP], lambda p: T.f0[:, CAP * r:CAP * r + CAP], "arr3", [whole("sb3")])
+    arrival("arr3", [("f0", 0, SL)])
     arrival("arrd", [("dall", 4, 12)])
-    tt(T.z3w[:, :], T.z3w[:, :], T.z1w[:, 0:128], A.min, [whole("z3w"), whole("z1w")], [whole("z3w")])
-    ts(T.l0[:, :], T.z3w[:, :], 0.25 - OFF, None, A.add, None, [whole("z3w")], [whole("l0")])
+    if CFG["c1late"]:
+        c1_scan()
+    cp(T.m2[:, 0:n].indirect(T.hu[:, 0:2]), T.pos[:, :], [whole("hu"), whole("pos")], [("m2", 0, n)])
+    merge = lambda: tt(T.z3w[:, :], T.z3w[:, :], T.z1w[:, 0:128], A.min, [whole("z3w"), whole("z1w")], [whole("z3w")])
+    offs0 = lambda: ts(T.l0[:, :], T.z3w[:, :], 0.25 - OFF, None, A.add, None, [whole("z3w")], [whole("l0")])
+    if CFG["l0e"]:
+        merge()
+    tt(T.p1[:, :], T.c1[:, :], T.t1[:, :], A.add, [whole("c1"), whole("t1")], [whole("p1")])
+    if CFG["l0e"]:
+        offs0()
+    op("v", lambda: V.tensor_reduce(T.dd[:, 0:1], T.dall[:, 0:11], AxisListType.X, A.max), [whole("dall")], [whole("dd")])
 
-    fin = CFG["fin"]
-
-    def x_gather(k):
-        lo, hi = fin[k]
-        tt(T.x0[:, lo:hi], T.f0[:, :].indirect(T.l0[:, lo // 16:hi // 16]), T.f1[:, lo:hi], A.add,
-           [whole("f0"), whole("l0"), ("f1", lo, hi)], [("x0", lo, hi)])
-
-    def m_scan(k):
-        lo, hi = fin[k]
-        init = 0.0 if k == 0 else T.mx[:, hi:hi + 1]
-        scan(rev("mx", lo, hi), rev("m0", lo + 1, hi + 1), rev("x0", lo, hi), init, A.mult, A.max,
-             [whole("m0"), ("x0", lo, hi)] + ([] if k == 0 else [("mx", hi, hi + 1)]), [("mx", lo, hi)])
-
-    def slack(q, out, src, lo, hi, at):
+    def rest(q, out, src, rd, wr):
         if q == "s":
-            act(T[out][:, lo:hi], T[src][:, lo:hi], AF.Identity, [(src, lo, hi), whole("dd")], [(out, lo, hi)], bias=T.dd[:, 0:1], scale=-1.0)
+            act(out, src, AF.Identity, rd + [whole("dd")], wr, bias=T.dd[:, 0:1], scale=-1.0)
         else:
-            ts(T[out][:, lo:hi], T[src][:, lo:hi], -1.0, T.dd[:, 0:1], A.mult, A.add, [(src, lo, hi), whole("dd")], [(out, lo, hi)])
-        dma("y", T.y[:, at + lo:at + hi], T[out][:, lo:hi], [(out, lo, hi)], [("y", at + lo, at + hi)])
+            ts(out, src, -1.0, T.dd[:, 0:1], A.mult, A.add, rd + [whole("dd")], wr)
+    if not CFG["l0e"]:
+        merge()
+    for k, q in enumerate(CFG["y1q"]):
+        lo, hi = k * n // len(CFG["y1q"]) // 32 * 32, (k + 1) * n // len(CFG["y1q"]) // 32 * 32
+        rest(q, T.p1[:, lo:hi], T.p1[:, lo:hi], [("p1", lo, hi)], [("p1", lo, hi)])
+        dma("y", T.y[:, n + lo:n + hi], T.p1[:, lo:hi], [("p1", lo, hi)], [("y", n + lo, n + hi)])
+    if not CFG["l0e"]:
+        offs0()
 
-    def end_of_plan():
-        op("v", lambda: V.tensor_reduce(T.dd[:, 0:1], T.dall[:, 0:11], AxisListType.X, A.max), [whole("dall")], [whole("dd")])
-    x_gather(0)
-    if CFG["dpos"] == 0:
-        end_of_plan()
-    halves = [(0, n // 2), (n // 2, n)]
-    for k in range(len(fin)):
-        if k + 1 < len(fin):
-            x_gather(k + 1)
-        m_scan(k)
-        if k + 1 == CFG["dpos"]:
-            end_of_plan()
-    for k in range(len(fin)):
-        if k < len(halves):
-            slack("s", "p1", "p1", halves[k][0], halves[k][1], n)
-        slack("s" if k + CFG["vact"] < len(fin) else "v", "x0", "mx", fin[k][0], fin[k][1], 0)
+    fq = CFG["fq"]
+    for lo, hi, q in fq:
+        if q == "s":
+            rest(q, T.x0[:, lo:hi], T.f0[:, :].indirect(T.l0[:, lo // 16:hi // 16]), [whole("f0"), whole("l0")], [("x0", lo, hi)])
+    top = n
+    for k, (lo, hi, q) in enumerate(fq):
+        if q == "v":
+            rest(q, T.x0[:, lo:hi], T.f0[:, :].indirect(T.l0[:, lo // 16:hi // 16]), [whole("f0"), whole("l0")], [("x0", lo, hi)])
+        init = BIG if k == 0 else T.mx[:, hi:hi + 1]
+        scan(rev("mx", lo, hi), rev("m2", lo + 1, hi + 1), rev("x0", lo, hi), init, A.max, A.min,
+             [whole("m2"), ("x0", lo, hi)] + ([] if k == 0 else [("mx", hi, hi + 1)]), [("mx", lo, hi)])
+        if k in CFG["st"]:
+            dma("y", T.y[:, lo:top], T.mx[:, lo:top], [("mx", lo, top)], [("y", lo, top)])
+            top = lo
     op("y", None, [("y", 0, 2 * n)], [])
 
     def meet(a, b):

@@ -4,35 +4,42 @@ from concourse.mybir import AluOpType as A, AxisListType, ActivationFunctionType
 n, CAP, NR = 2048, 192, 8
 SL = NR * CAP
 W = n + SL
+ZW = n + 1664
 BIG = float(1 << 20)
-FAR = 8192.0
 OFF = 512
-ZW = 3712
-CFG = {"q1": [(1536, 2048, "s"), (1024, 1536, "s"), (512, 1024, "s"), (0, 512, "s")], "vsend": 0, "shipa": 2, "s2a": 3,
-       "y1q": "sv", "l0e": 0, "vship": 0, "c1late": 1,
-       "fq": [(1664, 2048, "v"), (1152, 1664, "s"), (640, 1152, "s"), (256, 640, "s"), (0, 256, "s")], "st": [0, 1, 2, 3, 4]}
+EMPTY = (1 << 20) | 15
+U = 64
+CFG = {"loads": [("s", "hd", 0, 6), ("y", "d2", 1408, n), ("s", "pv", 0, 256), ("y", "d0", 0, n), ("y", "sh", 0, 192), ("y", "d2", 0, 1408)],
+       "silu": 1, "pe": 0, "pp": 1, "cmp": 1, "fg": 8,
+       "order": "kk warm mc m2 hu neg m2k m0z u8 pu2 a8 c32 su as7 q p u24 a24 p q p q p pu1 p q iv7 q pm m1 js4 jv3 pf r15 l1 r17 "
+                "es11 es13 es8 t11 C2 x11 b11 t13 C2 t8 x10 x11 Da11 la D b21 C28 l0 P16 dd pos P16 ys15 m0 yv9 ys8 hv5 hs10 hv3 hs9 hs5 z5 z13 z9 zs5",
+       "fs": [8, 8, 6, 4]}
 
 f32, bf, i32, u16 = "float32", "bfloat16", "int32", "uint16"
 SCRATCH = {k: ("sbuf", [128, c], d) for k, c, d in [
     ("pv", 256, i32), ("sh", 192, i32), ("hd", 8, i32), ("hu", 8, u16),
-    ("d0", n, bf), ("d2", n, bf), ("a1", n + 16, bf), ("d1", n, bf), ("m0", n + 16, bf), ("m2", n + 16, bf),
-    ("zer", 32, bf), ("neg", 32, bf), ("pos", 32, bf), ("far", 224, f32), ("j16", 128, f32), ("pi", 4, i32), ("pm", 4, i32), ("pf", 4, f32),
-    ("idw", 128, f32), ("val", W, f32), ("z1", W, f32), ("z2", ZW, f32), ("z3", ZW, f32),
-    ("z1w", 224, f32), ("z2w", 128, f32), ("z3w", 128, f32),
-    ("ty", 192, i32), ("tu", 192, i32), ("tz", 192, f32), ("tw", 192, f32), ("py", 128, i32), ("pz", 128, f32), ("pw", 128, f32),
-    ("pu", 256, u16), ("su", 96, u16), ("so", 192, u16), ("po", 128, u16), ("l1", 128, u16), ("l0", 128, u16), ("ls", 96, u16),
-    ("f1", W, f32), ("w2", W + SL, f32), ("f0", W, f32), ("u2", n, f32), ("r1", n, f32), ("q1", n, f32), ("c1", n, f32),
-    ("p1", n, f32), ("x0", n, f32), ("mx", n, f32), ("sb1", SL, f32), ("sb3", SL, f32), ("dall", 12, f32), ("dd", 4, f32)]}
+    ("d0", n, bf), ("d2", n, bf), ("d1", n, bf), ("a1", n + 16, bf), ("mc", n + 16, bf), ("m0", n + 16, bf), ("m2", n + 16, bf),
+    ("zer", 32, bf), ("neg", 32, bf), ("pos", 32, bf), ("kk", 32, bf), ("j16", 192, f32), ("idt", 128, f32),
+    ("one", 128, bf), ("eyf", 128, f32), ("eyb", 128, bf), ("ts1", n, f32),
+    ("pj", 4, i32), ("pm", 4, i32), ("pf", 4, f32),
+    ("val", SL, f32), ("z2s", ZW, f32), ("z2v", ZW, f32), ("z3s", ZW, f32), ("z3v", ZW, f32),
+    ("z2sw", 128, f32), ("z2vw", 128, f32), ("z3sw", 128, f32), ("z3vw", 128, f32),
+    ("ty", 192, i32), ("tz", 192, f32), ("tw", 192, f32),
+    ("pu", 256, u16), ("su", 96, u16), ("so", 192, u16), ("l0", 128, u16), ("l1", 128, u16),
+    ("f1", W, f32), ("w2", W + SL, f32), ("f0", W + SL, f32), ("u2", n, f32), ("r1", n, f32), ("q1", n, f32), ("c1", n, f32),
+    ("p1", n, f32), ("x1", n, f32), ("dall", W // 2 + 8, f32), ("dd", 4, f32)]}
 SCRATCH["t1"] = ("psum", [128, n], f32)
-SEMAPHORES = ["e%d" % k for k in range(130)] + ["arr1", "arr2", "arr3", "arrd", "sent"]
+SCRATCH["pa"] = ("psum", [128, n], f32)
+SEMAPHORES = ["e%d" % k for k in range(100)] + ["arr1", "arr2", "arr3", "arrd", "out1", "out2", "out3", "outd"]
 
 
-def engine_sets(topo, src, peers):
+def engine_sets(topo, src, peers, share=1):
     eng = topo.engines(src, peers[0])
     far = [p for p in peers if topo.die(p) != topo.die(src)]
     near = [p for p in peers if topo.die(p) == topo.die(src)]
     res = {}
     for group, pool in ((far, eng[0::2]), (near, eng[1::2])):
+        pool = pool[:len(pool) // share]
         size = {p: 1 for p in group}
         grown = True
         while grown:
@@ -65,28 +72,38 @@ def rank_program(g, core, T, topo):
         return
     cores = list(T.cores)
     others = [p for p in range(NR) if p != r]
-    mine = engine_sets(topo, core, [cores[p] for p in others])
-    coming = sum(len(engine_sets(topo, cores[p], [c for c in cores if c != cores[p]])[core]) for p in others)
+    share = CFG.get("share", {"1": 1, "2": 1, "3": 1, "d": 1})
+    mine = {k: engine_sets(topo, core, [cores[p] for p in others], s) for k, s in share.items()}
+    going = {k: sum(len(e) for e in mine[k].values()) for k in share}
+    coming = {k: sum(len(engine_sets(topo, cores[p], [c for c in cores if c != cores[p]], s)[core]) for p in others) for k, s in share.items()}
+    if CFG.get("one"):
+        going["d"] = len(topo.engines(core, cores[others[0]]))
+        coming["d"] = sum(len(topo.engines(cores[p], core)) for p in others)
     V, S, Y = g.vector, g.scalar, g.sync
-    Q = {"v": V, "s": S, "y": Y, "g": g}
+    Q = {"v": V, "s": S, "y": Y, "g": g, "t": g.tensor}
     ops = []
+    COPY = AF.Silu if CFG.get("silu") else AF.Copy
+    zer = "kk" if CFG.get("silu") else "zer"
 
     def op(q, fn, rd, wr, dma=False, sem=None):
         ops.append({"q": q, "fn": fn, "rd": rd, "wr": wr, "inc": 16 if dma else 1, "sem": sem})
 
-    def arrival(name, wr):
-        op("x", None, [], wr, sem=name)
-
-    def send(src, dst, sem, rd):
+    def send(src, dst, k, rd, lands, to=others):
         def fn():
             tr = []
-            for p in others:
+            if k == "d" and CFG.get("one"):
+                tr = [RemoteDMATransfer(dst_ids=[DstId(rid=topo.addr(cores[p])[0], pnc=topo.addr(cores[p])[1]) for p in others],
+                                        dma_engine_mask=topo.mask(core, cores[others[0]]), remote_sem=T.sem.arrd,
+                                        srcs=[src(r)], dsts=[dst(p) for p in others])]
+            for p in to if not tr else []:
                 rid, pid, _ = topo.addr(cores[p])
-                tr.append(RemoteDMATransfer(dst_ids=[DstId(rid=rid, pnc=pid)], dma_engine_mask=sum(1 << e for e in mine[cores[p]]),
-                                            remote_sem=T.sem[sem], src=src(p), dst=dst(p)))
-            g.remote_dma_fused(tr, local_sem=T.sem.sent)
+                tr.append(RemoteDMATransfer(dst_ids=[DstId(rid=rid, pnc=pid)], dma_engine_mask=sum(1 << e for e in mine[k][cores[p]]),
+                                            remote_sem=T.sem["arr" + k], src=src(p), dst=dst(p)))
+            g.remote_dma_fused(tr, local_sem=T.sem["out" + k])
             return None
         op("g", fn, rd, [])
+        if lands:
+            op("x", None, [], lands, sem=("arr" + k, coming[k]))
 
     def ts(out, a, s1, s2, o0, o1, rd, wr):
         if o1 is None:
@@ -112,11 +129,11 @@ def rank_program(g, core, T, topo):
     def fill(name, lo, hi, c):
         op("v", lambda: V.memset(T[name][:, lo:hi], c), [], [(name, lo, hi)])
 
-    def iota(name, lo, hi, step, base, mult, flt=True):
-        if flt:
-            op("g", lambda: g.iota(T[name][:, lo:hi], [[step, hi - lo]], base, mult, allow_small_or_imprecise_dtypes=True), [], [(name, lo, hi)])
-        else:
+    def iota(name, lo, hi, step, base, mult):
+        if SCRATCH[name][2] == i32:
             op("g", lambda: g.iota(T[name][:, lo:hi], [[step, hi - lo]], base, mult), [], [(name, lo, hi)])
+        else:
+            op("g", lambda: g.iota(T[name][:, lo:hi], [[step, hi - lo]], base, mult, allow_small_or_imprecise_dtypes=True), [], [(name, lo, hi)])
 
     def rev(name, lo, hi):
         return T[name][:, hi - 1::-1] if lo == 0 else T[name][:, hi - 1:lo - 1:-1]
@@ -130,181 +147,426 @@ def rank_program(g, core, T, topo):
         if q == "v":
             cp(T[out][:, olo:ohi], src, [(win, wlo, whi), (off, clo, chi)], [(out, olo, ohi)])
         else:
-            act(T[out][:, olo:ohi], src, AF.Copy, [(win, wlo, whi), (off, clo, chi)], [(out, olo, ohi)])
+            act(T[out][:, olo:ohi], src, COPY, [(win, wlo, whi), (off, clo, chi)], [(out, olo, ohi)])
 
-    def ship_places(lo):
-        hi = lo + 96
+    def scatter(q, win, wlo, whi, off, clo, chi, src, slo):
+        out, shi = T[win][:, wlo:whi].indirect(T[off][:, clo:chi]), slo + 16 * (chi - clo)
+        if q == "v":
+            cp(out, T[src][:, slo:shi], [(off, clo, chi), (src, slo, shi)], [(win, wlo, whi)])
+        else:
+            act(out, T[src][:, slo:shi], AF.Silu, [(off, clo, chi), (src, slo, shi)], [(win, wlo, whi)])
+
+    def mark(name, stage, const):
+        scatter("v", name, 0, n, "hu", 2 * stage, 2 * stage + 2, const, 0)
+
+    a_ = lambda name: T[name][:, :]
+
+    def ship_places(lo, hi):
         a = lambda name: T[name][:, lo:hi]
+        if CFG.get("pp"):
+            z, w = ("t1", lo, hi), ("t1", 256 + lo, 256 + hi)
+        else:
+            z, w = ("tz", lo, hi), ("tw", lo, hi)
+        b = lambda x: T[x[0]][:, x[1]:x[2]]
         return [
-            lambda: ts(a("ty"), a("sh"), 15, None, A.bitwise_and, None, [("sh", lo, hi)], [("ty", lo, hi)]),
-            lambda: ts(a("tu"), a("sh"), 65535, None, A.bitwise_and, None, [("sh", lo, hi)], [("tu", lo, hi)]),
-            lambda: ts(a("tz"), a("ty"), 2047.0, None, A.mult, None, [("ty", lo, hi)], [("tz", lo, hi)]),
-            lambda: tt(a("tw"), a("tu"), a("tz"), A.add, [("tu", lo, hi), ("tz", lo, hi)], [("tw", lo, hi)]),
-            lambda: tt(a("tz"), a("tw"), T.j16[:, 0:96], A.min, [("tw", lo, hi), ("j16", 0, 96)], [("tz", lo, hi)]),
+            lambda: ts(a("ty"), a("sh"), EMPTY, None, A.bitwise_and, None, [("sh", lo, hi)], [("ty", lo, hi)]),
+            lambda: ts(b(z), a("ty"), 2047.0, None, A.mult, None, [("ty", lo, hi)], [z]),
+            lambda: tt(b(w), a("sh"), b(z), A.add, [("sh", lo, hi), z], [w]),
+            lambda: tt(a("tz"), b(w), a("j16"), A.min, [w, whole("j16")], [("tz", lo, hi)]),
             lambda: ts(a("so"), a("tz"), 0.0625, None, A.mult, None, [("tz", lo, hi)], [("so", lo, hi)])]
 
-    def ship_inverse(z, lo, slots, q="s"):
-        for a, b in runs(slots):
-            out, rd = T[z][:, 0:ZW].indirect(T.so[:, lo + 12 * a:lo + 12 * b]), [("so", lo + 12 * a, lo + 12 * b), ("val", CAP * a, CAP * b)]
-            if q == "s":
-                act(out, T.val[:, CAP * a:CAP * b], AF.Silu, rd, [whole(z)])
-            else:
-                cp(out, T.val[:, CAP * a:CAP * b], rd, [whole(z)])
+    order = CFG["order"].split()
+    total = lambda head: sum(int(x[len(head):]) for x in order if x[:len(head)] == head and x[len(head):].isdigit())
+    at = {}
 
-    dma("s", T.sh[:, :], T.ship[:, :], [], [whole("sh")])
-    dma("s", T.hd[:, 0:6], T.heads[:, :], [], [whole("hd")])
-    dma("y", T.pv[:, :], T.prev[:, :], [], [whole("pv")])
-    iota("val", 0, 512, 1, OFF, 0)
-    iota("j16", 0, 128, 256, 16 * n, 16)
-    iota("pi", 0, 1, 0, 0, 1, flt=False)
-    iota("val", 1024, SL, 1, OFF + 1024, 0)
-    iota("val", SL, W, 1, OFF + SL, 0)
-    fill("far", 0, 224, FAR)
-    dma("y", T.z2[0:128:16, 0:n], T.far[:, 0:128], [whole("far")], [("z2", 0, n)])
-    dma("y", T.d0[:, :], T.dur[:, 0:n], [], [whole("d0")])
-    dma("y", T.d2[:, :], T.dur[:, 2 * n:3 * n], [], [whole("d2")])
-    dma("y", T.z1[0:128:16, :], T.far[:, :], [whole("far")], [whole("z1")])
-    fill("zer", 0, 32, 0.0)
-    fill("neg", 0, 32, -BIG)
-    fill("pos", 0, 32, BIG)
-    fill("dall", 0, 4, 0.0)
-    fill("m0", 0, n + 16, 1.0)
-    fill("m2", 0, n + 16, 1.0)
-    act(T.val[:, 512:1024], T.val[:, 0:512], AF.Silu, [("val", 0, 512)], [("val", 512, 1024)], bias=512.0)
-    dma("y", T.w2[:, W:W + SL], T.val[:, 0:SL], [("val", 0, SL)], [("w2", W, W + SL)])
-    dma("y", T.a1[:, :], T.dur[:, n:2 * n + 16], [], [whole("a1")])
-    dma("y", T.d1[:, :], T.dur[:, n:2 * n], [], [whole("d1")])
-    dma("y", T.z3[0:128:16, 0:n], T.far[:, 0:128], [whole("far")], [("z3", 0, n)])
+    def down(key, k):
+        hi = at.get(key, n)
+        at[key] = hi - U * k
+        return hi - U * k, hi
 
-    sp = ship_places(96)
-    sp[0](); sp[1](); sp[2]()
-    cp(T.su[:, :], T.sh[:, 0:96], [("sh", 0, 96)], [whole("su")])
-    sp[3]()
-    cp(T.hu[:, 0:6], T.hd[:, 0:6], [whole("hd")], [whole("hu")])
-    sp[4]()
-    cp(T.m0[:, 0:n].indirect(T.hu[:, 0:2]), T.zer[:, :], [whole("hu"), whole("zer")], [("m0", 0, n)])
-    sp[5]()
-    ship_inverse("z2", 96, others[:CFG["s2a"]])
-    cp(T.m2[:, 0:n].indirect(T.hu[:, 4:6]), T.zer[:, :], [whole("hu"), whole("zer")], [("m2", 0, n)])
-    ts(T.py[:, :], T.pv[:, 0:128], 15, None, A.bitwise_and, None, [("pv", 0, 128)], [whole("py")])
-    scan(T.f1[:, 0:n], T.m0[:, 0:n], T.d0[:, :], 0.0, A.mult, A.add, [whole("m0"), whole("d0")], [("f1", 0, n)])
-    ts(T.pz[:, :], T.py[:, :], 3583.0, None, A.mult, None, [whole("py")], [whole("pz")])
-    cp(T.pu[:, :], T.pv[:, :], [whole("pv")], [whole("pu")])
-    tt(T.pw[:, :], T.pv[:, 0:128], T.pz[:, :], A.add, [("pv", 0, 128), whole("pz")], [whole("pw")])
-    scan(rev("u2", 0, n), rev("m2", 1, n + 1), rev("d2", 0, n), 0.0, A.mult, A.add, [whole("m2"), whole("d2")], [whole("u2")])
-    ts(T.po[:, :], T.pw[:, :], 0.0625, None, A.mult, None, [whole("pw")], [whole("po")])
-    for a, b in runs(others):
-        gather("s", "sb1", CAP * a, "f1", 0, n, "su", 12 * a, 12 * b)
-    send(lambda p: T.sb1[:, CAP * p:CAP * p + CAP], lambda p: T.f1[:, n + CAP * r:n + CAP * r + CAP], "arr1", [whole("sb1")])
-    ship_inverse("z2", 96, others[CFG["s2a"]:])
-    dma("y", T.z2w[:, :], T.z2[0:128:16, 0:n], [("z2", 0, n)], [whole("z2w")])
-    act(T.z1[:, :].indirect(T.po[:, :]), T.val[:, SL:W], AF.Silu, [whole("po"), ("val", SL, W)], [whole("z1")])
-    dma("y", T.z1w[:, :], T.z1[0:128:16, :], [whole("z1")], [whole("z1w")])
-    cp(T.w2[:, SL:SL + W].indirect(T.pu[:, 128:256]), T.u2[:, :], [("pu", 128, 256), whole("u2")], [("w2", SL, SL + W)])
-    send(lambda p: T.w2[:, W + CAP * p:W + CAP * p + CAP], lambda p: T.w2[:, CAP * r:CAP * r + CAP], "arr2", [("w2", W, W + SL)])
-    iota("m2", 0, n + 16, 0, 0, 0)
-    arrival("arr1", [("f1", n, W)])
-    arrival("arr2", [("w2", 0, SL)])
+    def up(key, k):
+        lo = at.get(key, 0)
+        at[key] = lo + U * k
+        return lo, lo + U * k
 
-    sp = ship_places(0)
-    sp[0](); sp[1]()
-    ts(T.pm[:, 0:1], T.pi[:, 0:1], 112, None, A.bitwise_and, None, [whole("pi")], [whole("pm")])
-    sp[2]()
-    cp(T.pf[:, 0:1], T.pm[:, 0:1], [whole("pm")], [whole("pf")])
-    sp[3]()
-    ts(T.idw[:, :], T.j16[:, :], 0.0625, T.pf[:, 0:1], A.mult, A.subtract, [whole("j16"), whole("pf")], [whole("idw")])
-    sp[4]()
-    tt(T.idw[:, :], T.idw[:, :], T.z2w[:, :], A.min, [whole("idw"), whole("z2w")], [whole("idw")])
-    sp[5]()
-    ts(T.l1[:, :], T.idw[:, :], 0.25 - OFF, None, A.add, None, [whole("idw")], [whole("l1")])
-    cp(T.a1[:, :].indirect(T.hu[:, 2:4]), T.neg[:, :], [whole("hu"), whole("neg")], [whole("a1")])
-    nv, na = CFG["vship"], CFG["vship"] + CFG["shipa"]
-    ship_inverse("z3", 0, others[:nv], "v")
-    ship_inverse("z3", 0, others[nv:na])
-    tt(T.r1[:, :], T.f1[:, :].indirect(T.pu[:, 0:128]), T.d1[:, :], A.add, [whole("f1"), ("pu", 0, 128), whole("d1")], [whole("r1")])
+    def slots(key, k):
+        lo = at.get(key, 0)
+        at[key] = lo + k
+        return [[lo, lo + k]] if cmp else runs(others[lo:lo + k])
 
-    def c1_scan():
-        scan(T.c1[:, :], T.a1[:, 0:n], T.r1[:, :], 0.0, A.add, A.max, [whole("a1"), whole("r1")], [whole("c1")])
-    if not CFG["c1late"]:
-        c1_scan()
+    def need(ok):
+        assert ok
 
-    ch = CFG["q1"]
+    m2 = "m2" if "m2" in order else "mc"
+    cmp = CFG.get("cmp")
+    LS = 84 if cmp else 96
+    here = (lambda p: p - (p > r)) if cmp else (lambda p: p)
+    there = (lambda p: r - (r > p)) if cmp else (lambda p: r)
+    sp2, sp1, spw = ship_places(LS, 2 * LS), ship_places(0, LS), ship_places(0, 2 * LS)
+    h = n // 2
+
+    def u2_scan(k):
+        lo, hi = down("u", k)
+        scan(rev("u2", lo, hi), rev(m2, lo + 1, hi + 1), rev("d2", lo, hi), float(OFF) if hi == n else T.u2[:, hi:hi + 1], A.min, A.add,
+             [whole(m2), ("d2", lo, hi)] + ([] if hi == n else [("u2", hi, hi + 1)]), [("u2", lo, hi)])
+
+    def u2_scatter(k):
+        lo, hi = down("a", k)
+        need(lo >= at["u"] and at.get("f", SL) + U * CFG.get("fg", 0) >= SL)
+        scatter("s", "w2", SL, SL + W, "pu", 128 + lo // 16, 128 + hi // 16, "u2", lo)
+        if lo == 0:
+            send(lambda p: T.w2[:, W + CAP * p:W + CAP * p + CAP], lambda p: T.w2[:, CAP * there(p):CAP * there(p) + CAP], "2", [("w2", W, W + SL)], [("w2", 0, SL)])
+            late_constants()
+
+    def c0_scan(k):
+        lo, hi = up("c", k)
+        scan(T[cw][:, co + lo:co + hi], T.mc[:, lo:hi], T.d0[:, lo:hi], float(OFF) if lo == 0 else T[cw][:, co + lo - 1:co + lo], A.min, A.add,
+             [whole("mc"), ("d0", lo, hi)] + ([] if lo == 0 else [(cw, co + lo - 1, co + lo)]), [(cw, co + lo, co + hi)])
+
+    cw, co, sb, so = ("f0", SL, "f1", 0) if "cut" in CFG else ("f1", 0, "f0", W)
+
+    def ship_gather(q, k):
+        need(at["c"] == n)
+        if CFG.get("two"):
+            first = sorted(others, key=lambda p: topo.die(cores[p]) == topo.die(core))
+            far = [p for p in others if topo.die(cores[p]) != topo.die(core)]
+            lo = at.get("A", 0)
+            at["A"] = lo + k
+            for a, b in runs(sorted(here(p) for p in first[lo:lo + k])):
+                gather(q, sb, so + CAP * a, cw, co, co + n, "su", 12 * a, 12 * b)
+            for to, end in ((far, len(far)), (first[len(far):], NR - 1)):
+                if lo < end <= lo + k:
+                    send(lambda p: T[sb][:, so + CAP * here(p):so + CAP * here(p) + CAP], lambda p: T[cw][:, co + n + CAP * r:co + n + CAP * r + CAP], "1",
+                         [(sb, so + CAP * here(p), so + CAP * here(p) + CAP) for p in to], [(cw, co + n, co + W)] if end == NR - 1 else None, to)
+            if at["A"] == NR - 1:
+                op("x", None, [], [("f0", W, W + SL)], sem=("out1", going["1"]))
+                late_constants()
+            return
+        for a, b in slots("A", k):
+            gather(q, sb, so + CAP * a, cw, co, co + n, "su", 12 * a, 12 * b)
+        if at["A"] == NR - 1:
+            send(lambda p: T[sb][:, so + CAP * here(p):so + CAP * here(p) + CAP], lambda p: T[cw][:, co + n + CAP * r:co + n + CAP * r + CAP], "1",
+                 [(sb, so, so + SL)], [(cw, co + n, co + W)])
+            if sb == "f0":
+                op("x", None, [], [("f0", W, W + SL)], sem=("out1", going["1"]))
+            late_constants()
+
+    def late_constants():
+        if at.get("A") == NR - 1 and at.get("a") == 0:
+            iota("m0", 0, n + 16, 0, 0, 0)
+
+    def ship_inverse(z, lo, key, q, k):
+        need(not (sp2 if lo else sp1))
+        for a, b in slots(key, k):
+            scatter(q, z + q, 0, ZW, "so", lo + 12 * a, lo + 12 * b, "val", CAP * a)
+        at[key + q] = at.get(key + q, 0) + k
+        if at[key + q] == total(key + q):
+            dma("y", a_(z + q + "w"), T[z + q][0:128:16, 0:n], [(z + q, 0, n)], [whole(z + q + "w")])
+
+    def offsets(l, z, key, half=False):
+        need(at[key] == NR - 1)
+        parts = [z + q + "w" for q in "sv" if total(key + q)]
+        if len(parts) == 2 and l + "a" not in at:
+            tt(a_(parts[0]), a_(parts[0]), a_(parts[1]), A.min, [whole(parts[0]), whole(parts[1])], [whole(parts[0])])
+        if half:
+            need(l not in at)
+            at[l + "a"] = 1
+            return
+        ts(a_(l), a_(parts[0]), T.pf[:, 0:1], None, A.subtract, None, [whole(parts[0]), whole("pf")], [whole(l)])
+        at[l] = 1
+
+    pe = CFG.get("pe")
+    t1, r1, rkey, p1 = ("ts1", "pa", "R", "t1") if pe else ("t1", "r1", "r", "p1")
+
+    def r1_gather(k, q="v"):
+        lo, hi = down("r", k)
+        need(at["A"] == NR - 1)
+        if pe:
+            gather(q, "r1", lo, "f1", 0, W, "pu", lo // 16, hi // 16)
+        else:
+            need(q == "v")
+            tt(T.r1[:, lo:hi], T[cw][:, co:co + W].indirect(T.pu[:, lo // 16:hi // 16]), T.d1[:, lo:hi], A.add,
+               [(cw, co, co + W), ("pu", 0, 128), whole("d1")], [("r1", lo, hi)])
+
+    def pass_on(out, src, eye, lo, hi, start, stop):
+        op("t", lambda: g.tensor.matmul(T[out][:, lo:hi], a_(eye), T[src][:, lo:hi], start, stop), [whole(eye), (src, lo, hi)], [(out, lo, hi)])
+
+    def d1_pe():
+        for lo in range(n - 512, -1, -512):
+            pass_on("pa", "d1", "eyb", lo, lo + 512, True, False)
+
+    def r1_pe():
+        lo, hi = down("R", 8)
+        need(lo >= at["r"] and at["dpe"])
+        pass_on("pa", "r1", "eyf", lo, hi, False, True)
+
+    def t1_pe():
+        lo, hi = down("T", 8)
+        need(lo >= at["t"])
+        pass_on("t1", "ts1", "eyf", lo, hi, True, False)
+
+    def c1_pe():
+        lo, hi = up("P", 8)
+        need(hi <= at["C"] and at["T"] == 0)
+        pass_on("t1", "c1", "eyf", lo, hi, False, True)
+
+    def eyes():
+        fill("one", 0, 128, 1.0)
+        for e in ("eyf", "eyb"):
+            op("g", lambda e=e: g.affine_select(a_(e), a_("one"), [[-1, 128]], A.is_equal, 0.0, 0, 1), [whole("one")], [whole(e)])
+
+    cut = U * CFG.get("cut", 0)
+    fused = "cut" in CFG
+
+    def side(lo, hi):
+        need(lo >= cut or hi <= cut)
+        return ("t1", "c1") if lo >= cut else ("ts1", "t1")
+
+    def t1_scan_f(k):
+        lo, hi = down("t", k)
+        need(lo >= at["e"] and at["m1"])
+        o, i = side(lo, hi)[0], side(hi, hi + 1)[0]
+        scan(rev(o, lo, hi), rev("a1", lo + 1, hi + 1), rev("q1", lo, hi), -BIG if hi == n else T[i][:, hi:hi + 1], A.add, A.max,
+             [("q1", lo, hi), whole("a1")] + ([] if hi == n else [(i, hi, hi + 1)]), [(o, lo, hi)])
+
+    def x1_scatter_f(k):
+        lo, hi = down("b", k)
+        need(at["r"] == 0)
+        if side(lo, hi)[0] == "t1":
+            need(lo >= at["x"])
+            scatter("s", "f0", SL, SL + W, "pu", lo // 16, hi // 16, "x1", lo)
+        else:
+            need(lo >= at["t"])
+            tt(T.f0[:, SL:SL + W].indirect(T.pu[:, lo // 16:hi // 16]), T.ts1[:, lo:hi], T.r1[:, lo:hi], A.add,
+               [("ts1", lo, hi), ("r1", lo, hi), ("pu", 0, 128)], [("f0", SL, SL + W)])
+        if lo == 0:
+            send(lambda p: T.f0[:, W + CAP * p:W + CAP * p + CAP], lambda p: T.f0[:, CAP * r:CAP * r + CAP], "3", [("f0", W, W + SL)], [("f0", 0, SL)])
+
+    def c1_scan_f(k):
+        lo, hi = up("C", k)
+        need(at["r"] == 0 and at["m1"] and not sp1 and not sp2)
+        o, i = side(lo, hi)[1], side(lo - 1, lo)[1]
+        scan(T[o][:, lo:hi], T.a1[:, lo:hi], T.r1[:, lo:hi], 0.0 if lo == 0 else T[i][:, lo - 1:lo], A.add, A.max,
+             [whole("a1"), whole("r1")] + ([] if lo == 0 else [(i, lo - 1, lo)]), [(o, lo, hi)])
+
+    def p1_add_f(k):
+        lo, hi = up("P", k)
+        need(hi <= at["C"] and at["t"] == 0)
+        a, b = side(lo, hi)
+        tt(T.p1[:, lo:hi], T[a][:, lo:hi], T[b][:, lo:hi], A.add, [(a, lo, hi), (b, lo, hi)], [("p1", lo, hi)])
+
+    def own_end_f(name, lo, half):
+        need(at["b"] == 0 if name == "f0" else at["P"] == n and "y" not in at)
+        at["D"] = half
+        scan(T.dall[:, 0:half], T[name][:, lo:lo + half], T[name][:, lo + half:lo + 2 * half], 0.0, A.max, A.max, [(name, lo, lo + 2 * half)], [("dall", 0, half)])
+        place = lambda p: half + (r if r < p else r - 1)
+        send(lambda p: T.dall[:, half - 1:half], lambda p: T.dall[:, place(p):place(p) + 1], "d", [("dall", 0, half)], [("dall", half, half + 8)])
+
+    def q1_gather(q, k):
+        lo, hi = down("e", k)
+        need(at["l1"] and at["a"] == 0)
+        gather(q, "q1", lo, "w2", 0, W, "l1", lo // 16, hi // 16)
+
+    def t1_scan(k):
+        lo, hi = down("t", k)
+        need(lo >= at["e"] and at["m1"])
+        scan(rev(t1, lo, hi), rev("a1", lo + 1, hi + 1), rev("q1", lo, hi), -BIG if hi == n else T[t1][:, hi:hi + 1], A.add, A.max,
+             [("q1", lo, hi), whole("a1")] + ([] if hi == n else [(t1, hi, hi + 1)]), [(t1, lo, hi)])
 
     def x1_add(k):
-        lo, hi, _ = ch[k]
-        tt(T.f0[:, SL + lo:SL + hi], T.r1[:, lo:hi], T.t1[:, lo:hi], A.add, [("r1", lo, hi), ("t1", lo, hi)], [("f0", SL + lo, SL + hi)])
-    for k, (lo, hi, q) in enumerate(ch):
-        gather(q, "q1", lo, "w2", 0, W, "l1", lo // 16, hi // 16)
-    for k, (lo, hi, q) in enumerate(ch):
-        init = -BIG if k == 0 else T.t1[:, hi:hi + 1]
-        scan(rev("t1", lo, hi), rev("a1", lo + 1, hi + 1), rev("q1", lo, hi), init, A.add, A.max,
-             [("q1", lo, hi), whole("a1")] + ([] if k == 0 else [("t1", hi, hi + 1)]), [("t1", lo, hi)])
-        if k > 0:
-            x1_add(k - 1)
-        else:
-            ts(T.ls[:, :], T.z1w[:, 128:224], 0.25 - n, n - 0.75, A.add, A.min, [whole("z1w")], [whole("ls")])
-    x1_add(len(ch) - 1)
-    ship_inverse("z3", 0, others[na:])
-    dma("y", T.z3w[:, :], T.z3[0:128:16, 0:n], [("z3", 0, n)], [whole("z3w")])
-    for q, slots in (("s", others[CFG["vsend"]:]), ("v", others[:CFG["vsend"]])):
-        for a, b in runs(slots):
-            gather(q, "sb3", CAP * a, "f0", SL, W, "ls", 12 * a, 12 * b)
-    op("v", lambda: V.tensor_reduce(T.dall[:, 0:1], T.f0[:, SL:W], AxisListType.X, A.max), [("f0", SL, W)], [("dall", 0, 4)])
-    place = lambda p: 4 + (r if r < p else r - 1)
-    send(lambda p: T.dall[:, 0:1], lambda p: T.dall[:, place(p):place(p) + 1], "arrd", [("dall", 0, 4)])
-    send(lambda p: T.sb3[:, CAP * p:CAP * p + CAP], lambda p: T.f0[:, CAP * r:CAP * r + CAP], "arr3", [whole("sb3")])
-    arrival("arr3", [("f0", 0, SL)])
-    arrival("arrd", [("dall", 4, 12)])
-    if CFG["c1late"]:
-        c1_scan()
-    cp(T.m2[:, 0:n].indirect(T.hu[:, 0:2]), T.pos[:, :], [whole("hu"), whole("pos")], [("m2", 0, n)])
-    merge = lambda: tt(T.z3w[:, :], T.z3w[:, :], T.z1w[:, 0:128], A.min, [whole("z3w"), whole("z1w")], [whole("z3w")])
-    offs0 = lambda: ts(T.l0[:, :], T.z3w[:, :], 0.25 - OFF, None, A.add, None, [whole("z3w")], [whole("l0")])
-    if CFG["l0e"]:
-        merge()
-    tt(T.p1[:, :], T.c1[:, :], T.t1[:, :], A.add, [whole("c1"), whole("t1")], [whole("p1")])
-    if CFG["l0e"]:
-        offs0()
-    op("v", lambda: V.tensor_reduce(T.dd[:, 0:1], T.dall[:, 0:11], AxisListType.X, A.max), [whole("dall")], [whole("dd")])
+        lo, hi = down("x", k)
+        need(lo >= at["t"] and lo >= at[rkey])
+        tt(T.x1[:, lo:hi], T[r1][:, lo:hi], T[t1][:, lo:hi], A.add, [(r1, lo, hi), (t1, lo, hi)], [("x1", lo, hi)])
+
+    def x1_scatter(k):
+        lo, hi = down("b", k)
+        need(lo >= at["x"])
+        scatter("s", "f0", SL, SL + W, "pu", lo // 16, hi // 16, "x1", lo)
+        if lo == 0:
+            need(at["D"] and (at.get("last") or not cmp))
+            send(lambda p: T.f0[:, W + CAP * p:W + CAP * p + CAP], lambda p: T.f0[:, CAP * there(p):CAP * there(p) + CAP], "3", [("f0", W, W + SL)], [("f0", 0, SL)])
+
+    def own_part(k):
+        lo, hi = down("Da", k)
+        need(lo >= at["x"] and (lo > 0 or "D" in at))
+        a, m = (n - hi) // 2, (lo + hi) // 2
+        scan(T.dall[:, a:a + m - lo], T.x1[:, lo:m], T.x1[:, m:hi], 0.0 if a == 0 else T.dall[:, a - 1:a], A.max, A.max,
+             [("x1", lo, hi)] + ([("dall", a - 1, a)] if a else []), [("dall", a, a + m - lo)])
+
+    def own_end():
+        need(at["x"] == 0)
+        at["D"] = h
+        own_part(at.get("Da", n) // U)
+        place = lambda p: h + (r if r < p else r - 1)
+        send(lambda p: T.dall[:, h - 1:h], lambda p: T.dall[:, place(p):place(p) + 1], "d", [("dall", 0, h)], [("dall", h, h + 8)])
+
+    def c1_scan(k):
+        lo, hi = up("C", k)
+        need(at[rkey] == 0 and at["m1"])
+        scan(T.c1[:, lo:hi], T.a1[:, lo:hi], T[r1][:, lo:hi], 0.0 if lo == 0 else T.c1[:, lo - 1:lo], A.add, A.max,
+             [whole("a1"), whole(r1)] + ([] if lo == 0 else [("c1", lo - 1, lo)]), [("c1", lo, hi)])
+
+    def p1_add(k):
+        lo, hi = up("P", k)
+        need(hi <= at["C"] and at["t"] == 0)
+        tt(T.p1[:, lo:hi], T.c1[:, lo:hi], T.t1[:, lo:hi], A.add, [("c1", lo, hi), whole("t1")], [("p1", lo, hi)])
+
+    def plan_end():
+        need(at["D"])
+        at["dd"] = 1
+        e = at["D"]
+        op("v", lambda: V.tensor_reduce(T.dd[:, 0:1], T.dall[:, e - 1:e + 7], AxisListType.X, A.max), [whole("dall")], [whole("dd")])
 
     def rest(q, out, src, rd, wr):
+        need(at["dd"])
         if q == "s":
             act(out, src, AF.Identity, rd + [whole("dd")], wr, bias=T.dd[:, 0:1], scale=-1.0)
         else:
             ts(out, src, -1.0, T.dd[:, 0:1], A.mult, A.add, rd + [whole("dd")], wr)
-    if not CFG["l0e"]:
-        merge()
-    for k, q in enumerate(CFG["y1q"]):
-        lo, hi = k * n // len(CFG["y1q"]) // 32 * 32, (k + 1) * n // len(CFG["y1q"]) // 32 * 32
-        rest(q, T.p1[:, lo:hi], T.p1[:, lo:hi], [("p1", lo, hi)], [("p1", lo, hi)])
-        dma("y", T.y[:, n + lo:n + hi], T.p1[:, lo:hi], [("p1", lo, hi)], [("y", n + lo, n + hi)])
-    if not CFG["l0e"]:
-        offs0()
 
-    fq = CFG["fq"]
-    for lo, hi, q in fq:
-        if q == "s":
-            rest(q, T.x0[:, lo:hi], T.f0[:, :].indirect(T.l0[:, lo // 16:hi // 16]), [whole("f0"), whole("l0")], [("x0", lo, hi)])
-    top = n
-    for k, (lo, hi, q) in enumerate(fq):
+    def slack1(q, k):
+        lo, hi = up("y", k)
+        need(hi <= at["P"])
+        rest(q, T.p1[:, lo:hi], T[p1][:, lo:hi], [(p1, lo, hi)], [("p1", lo, hi)])
+        if not CFG.get("sep"):
+            store1("y", k)
+
+    def store1(q, k):
+        lo, hi = up("Y", k)
+        need(hi <= at["y"])
+        dma(q, T.y[:, n + lo:n + hi], T.p1[:, lo:hi], [("p1", lo, hi)], [("y", n + lo, n + hi)])
+
+    def store0(q, k):
+        lo, hi = down("Z", k)
+        need(lo >= at["z"])
+        dma(q, T.y[:, lo:hi], T.u2[:, lo:hi], [("u2", lo, hi)], [("y", lo, hi)])
+
+    def x0_gather(q, lo, hi):
+        need(at["l0"] and at["b"] == 0)
+        rest(q, T.q1[:, lo:hi], T.f0[:, 0:W].indirect(T.l0[:, lo // 16:hi // 16]), [("f0", 0, W), whole("l0")], [("q1", lo, hi)])
+
+    def x0_scalar():
+        at["gs"] = n - U * total("gv")
+        for k in CFG["fs"]:
+            x0_gather("s", *down("gs", k))
+
+    def slack0(k, q="y"):
+        lo, hi = down("z", k)
+        need(at["m0"] and (lo >= at["h"] if "h" in at else at["gs"] == 0 and at["gv"] == n - U * total("gv")))
+        scan(rev("u2", lo, hi), rev("m0", lo + 1, hi + 1), rev("q1", lo, hi), BIG if hi == n else T.u2[:, hi:hi + 1], A.max, A.min,
+             [whole("m0"), ("q1", lo, hi)] + ([] if hi == n else [("u2", hi, hi + 1)]), [("u2", lo, hi)])
+        if not CFG.get("sep"):
+            store0(q, k)
+
+    def warm():
+        fill("w2", W, W + 256, float(OFF))
+        act(T.w2[:, W + 256:W + 512], T.w2[:, W:W + 256], AF.Silu, [("w2", W, W + 256)], [("w2", W + 256, W + 512)])
+        act(T.w2[:, W + 512:W + 1024], T.w2[:, W:W + 512], COPY, [("w2", W, W + 512)], [("w2", W + 512, W + 1024)])
+
+    def spare(q, k):
+        lo, hi = up("f", k)
         if q == "v":
-            rest(q, T.x0[:, lo:hi], T.f0[:, :].indirect(T.l0[:, lo // 16:hi // 16]), [whole("f0"), whole("l0")], [("x0", lo, hi)])
-        init = BIG if k == 0 else T.mx[:, hi:hi + 1]
-        scan(rev("mx", lo, hi), rev("m2", lo + 1, hi + 1), rev("x0", lo, hi), init, A.max, A.min,
-             [whole("m2"), ("x0", lo, hi)] + ([] if k == 0 else [("mx", hi, hi + 1)]), [("mx", lo, hi)])
-        if k in CFG["st"]:
-            dma("y", T.y[:, lo:top], T.mx[:, lo:top], [("mx", lo, top)], [("y", lo, top)])
-            top = lo
+            fill("w2", W + lo, W + hi, float(OFF))
+        elif q == "g":
+            iota("w2", W + lo, W + hi, 0, OFF, 0)
+        else:
+            need(hi - lo <= lo)
+            act(T.w2[:, W + lo:W + hi], T.w2[:, W:W + hi - lo], AF.Silu, [("w2", W, W + hi - lo)], [("w2", W + lo, W + hi)])
+
+    def once(key, fn):
+        def run():
+            at[key] = 1
+            fn()
+        return run
+    plain = {
+        "warm": warm, "mc": lambda: fill("mc", 0, n + 16, BIG), "m2": lambda: fill("m2", 0, n + 16, BIG),
+        "fill": lambda: fill("w2", W + 1024, W + SL, float(OFF)),
+        "fills": lambda: act(T.w2[:, W + 1024:W + SL], T.w2[:, W:W + 512], COPY, [("w2", W, W + 512)], [("w2", W + 1024, W + SL)]),
+        "kk": lambda: fill("kk", 0, 32, float(OFF)), "pos": lambda: fill("pos", 0, 32, BIG), "zer": lambda: fill("zer", 0, 32, 0.0),
+        "neg": lambda: fill("neg", 0, 32, -BIG),
+        "hu": lambda: cp(T.hu[:, 0:6], T.hd[:, 0:6], [whole("hd")], [whole("hu")]),
+        "su": lambda: cp(T.su[:, 0:LS], T.sh[:, 0:LS], [("sh", 0, LS)], [whole("su")]),
+        "last": once("last", lambda: fill("f0", W + SL - CAP, W + SL, float(OFF))),
+        "pu1": lambda: cp(T.pu[:, 0:128], T.pv[:, 0:128], [("pv", 0, 128)], [("pu", 0, 128)]),
+        "pu2": lambda: cp(T.pu[:, 128:256], T.pv[:, 128:256], [("pv", 128, 256)], [("pu", 128, 256)]),
+        "pu": lambda: cp(a_("pu"), a_("pv"), [whole("pv")], [whole("pu")]),
+        "m0z": lambda: mark("mc", 0, zer), "m0b": lambda: mark("mc", 0, "pos"), "m2k": lambda: mark(m2, 2, "kk"), "m2b": lambda: mark("mc", 2, "pos"),
+        "m1": once("m1", lambda: mark("a1", 1, "neg")), "m0": once("m0", lambda: mark("m0", 0, "pos")),
+        "p": lambda: sp2.pop(0)(), "q": lambda: sp1.pop(0)(),
+        "pm": lambda: ts(T.pm[:, 0:1], T.pj[:, 0:1], 112, None, A.bitwise_and, None, [whole("pj")], [whole("pm")]),
+        "pf": lambda: ts(T.pf[:, 0:1], T.pm[:, 0:1], OFF - 0.25, None, A.add, None, [whole("pm")], [whole("pf")]),
+        "l1": lambda: offsets("l1", "z2", "i"), "l0": lambda: offsets("l0", "z3", "j"),
+        "la": lambda: offsets("l0", "z3", "j", True), "lb": lambda: offsets("l1", "z2", "i", True),
+        "eye": eyes, "dpe": once("dpe", d1_pe), "R": r1_pe, "T": t1_pe, "P": c1_pe, "w": lambda: (sp1.pop(0), sp2.pop(0), spw.pop(0)()),
+        "D": own_end, "dd": plan_end, "gs": x0_scalar}
+    counted = {
+        "u": u2_scan, "a": u2_scatter, "c": c0_scan, "as": lambda k: ship_gather("s", k), "av": lambda k: ship_gather("v", k),
+        "is": lambda k: ship_inverse("z2", LS, "i", "s", k), "iv": lambda k: ship_inverse("z2", LS, "i", "v", k),
+        "js": lambda k: ship_inverse("z3", 0, "j", "s", k), "jv": lambda k: ship_inverse("z3", 0, "j", "v", k),
+        "r": r1_gather, "rs": lambda k: r1_gather(k, "s"), "es": lambda k: q1_gather("s", k), "ev": lambda k: q1_gather("v", k), "t": t1_scan, "x": x1_add, "b": x1_scatter,
+        "C": c1_scan, "P": p1_add, "ys": lambda k: slack1("s", k), "yv": lambda k: slack1("v", k),
+        "gv": lambda k: x0_gather("v", *down("gv", k)), "z": slack0,
+        "Yy": lambda k: store1("y", k), "Ys": lambda k: store1("s", k), "Yg": lambda k: store1("g", k),
+        "Zy": lambda k: store0("y", k), "Zs": lambda k: store0("s", k), "Zg": lambda k: store0("g", k),
+        "Da": own_part, "zs": lambda k: slack0(k, "s"), "fv": lambda k: spare("v", k), "fs": lambda k: spare("s", k),
+        "hs": lambda k: x0_gather("s", *down("h", k)), "hv": lambda k: x0_gather("v", *down("h", k))}
+
+    if fused:
+        counted.update(t=t1_scan_f, b=x1_scatter_f, C=c1_scan_f, P=p1_add_f)
+        plain.update(Dw=lambda: own_end_f("f0", SL, W // 2), Dp=lambda: own_end_f("p1", 0, h), own=lambda: fill("f0", W + CAP * r, W + CAP * r + CAP, 0.0))
+
+    if "mc" not in order:
+        iota("mc", 0, n + 16, 0, int(BIG), 0)
+    if CFG.get("fg"):
+        iota("w2", W + SL - U * CFG["fg"], W + SL, 0, OFF, 0)
+    iota("pj", 0, 1, 0, 0, 1)
+    iota("idt", 0, 128, 16, n, 1)
+    if CFG.get("fg") and cmp:
+        at["last"] = 1
+        iota("f0", W + SL - CAP, W + SL, 0, OFF, 0)
+    loads = list(CFG["loads"])
+    if "a1" not in [x[1] for x in loads]:
+        loads += [("y", z, 0, n) for z in ("z2s", "z2v", "z3s", "z3v", "d1")] + [("y", "a1", 0, n + 16)]
+    for q, name, lo, hi in loads:
+        if name[0] == "z":
+            if total({"z2": "i", "z3": "j"}[name[:2]] + name[2]):
+                dma(q, T[name][0:128:16, 0:n], a_("idt"), [whole("idt")], [(name, 0, n)])
+            continue
+        if name == "sh" and cmp:
+            to = 0
+            for a, b in ((0, 12 * r), (12 * r + 12, 96 + 12 * r), (108 + 12 * r, 192)):
+                if b > a:
+                    dma(q, T.sh[:, to:to + b - a], T.ship[:, a:b], [], [("sh", to, to + b - a)])
+                to += b - a
+            continue
+        src, base = {"hd": (T.heads, 0), "pv": (T.prev, 0), "sh": (T.ship, 0), "d0": (T.dur, 0), "d2": (T.dur, 2 * n), "d1": (T.dur, n), "a1": (T.dur, n)}[name]
+        dma(q, T[name][:, lo:hi], src[:, base + lo:base + hi], [], [(name, lo, hi)])
+    op("g", lambda: g.iota(T.j16[:, 0:2 * LS], [[0, 2], [256, LS]], 16 * n, 16, allow_small_or_imprecise_dtypes=True), [], [whole("j16")])
+    for lo, hi in ([(0, SL - CAP)] if cmp else [(0, 4 * CAP), (4 * CAP, SL)] if CFG.get("val2") else [(0, SL)]):
+        iota("val", lo, hi, 1, OFF + lo, 1)
+    for x in order:
+        if x in plain:
+            plain[x]()
+        else:
+            head = x.rstrip("0123456789")
+            counted[head](int(x[len(head):]))
+    need(at["Z"] == 0 and at["Y"] == n)
     op("y", None, [("y", 0, 2 * n)], [])
 
     def meet(a, b):
         return any(x[0] == z[0] and x[1] < z[2] and z[1] < x[2] for x in a for z in b)
-    known = {q: set() for q in "vsygx"}
+    for o in ops:
+        o["bank"] = [(x[0], x[1] // 512 * 512, (x[2] + 511) // 512 * 512) for x in o["rd"] + o["wr"] if x[0] in ("t1", "pa")]
+    known = {q: set() for q in "vsygxt"}
     closure, waits, used = [], [], set()
     for k, o in enumerate(ops):
-        deps = [j for j in range(k) if meet(ops[j]["wr"], o["rd"] + o["wr"]) or meet(ops[j]["rd"], o["wr"])]
+        deps = [j for j in range(k) if meet(ops[j]["wr"], o["rd"] + o["wr"]) or meet(ops[j]["rd"], o["wr"])
+                or (ops[j]["q"] != o["q"] and meet(ops[j]["bank"], o["bank"]))]
         if o["q"] == "x":
             deps = []
+        deps = [j for j in deps if ops[j]["q"] != "g" or ops[j]["wr"]]
+        if CFG.get("free") and o["inc"] == 1 and o["q"] in "vs":
+            deps = [j for j in deps if ops[j]["q"] != o["q"] or ops[j]["inc"] != 1 or meet(ops[j]["wr"], o["rd"])]
         kn, w = known[o["q"]], []
         for j in sorted(deps, reverse=True):
             if j not in kn:
@@ -313,14 +575,24 @@ def rank_program(g, core, T, topo):
         waits.append(w)
         used |= set(w)
         closure.append((set() if o["q"] == "x" else set(kn)) | {k})
-    sems = {}
+    sems, lines = {}, []
     for j in sorted(used):
-        sems[j] = (T.sem[ops[j]["sem"]], coming) if ops[j]["sem"] else (T.sem["e%d" % len(sems)], ops[j]["inc"])
+        if ops[j]["sem"]:
+            sems[j] = (T.sem[ops[j]["sem"][0]], ops[j]["sem"][1])
+            continue
+        kind = (ops[j]["q"], ops[j]["inc"])
+        line = next((x for x in lines if x[0] == kind and x[1] in closure[j]), None)
+        if line is None:
+            line = [kind, j, 0, T.sem["e%d" % len(lines)]]
+            lines.append(line)
+        line[1], line[2] = j, line[2] + ops[j]["inc"]
+        sems[j] = (line[3], line[2])
     for k, o in enumerate(ops):
         for j in reversed(waits[k]):
             Q[o["q"]].wait_ge(sems[j][0], sems[j][1])
         if o["fn"] is not None:
             ins = o["fn"]()
             if k in sems:
-                ins.then_inc(sems[k][0], sems[k][1])
-    g.wait_ge(T.sem.sent, 4 * sum(len(e) for e in mine.values()))
+                ins.then_inc(sems[k][0], o["inc"])
+    for k in share:
+        g.wait_ge(T.sem["out" + k], going[k])

from concourse.bass import DstId, RemoteDMATransfer
from concourse.mybir import AluOpType as A, AxisListType, ActivationFunctionType as AF

n, CAP, NR = 2048, 192, 8
SL = NR * CAP
W = n + SL
ZW = n + 1664
BIG = float(1 << 20)
OFF = 512
EMPTY = (1 << 20) | 15
U = 64
CFG = {"loads": [("s", "hd", 0, 6), ("y", "d2", 1408, n), ("s", "pv", 0, 256), ("y", "d0", 0, n), ("y", "sh", 0, 192), ("y", "d2", 0, 1408)],
       "silu": 1, "pe": 0, "pp": 1, "cmp": 1, "fg": 8,
       "order": "kk warm mc m2 hu neg m2k m0z u8 pu2 a8 c32 su as7 q p u24 a24 p q p q p pu1 p q iv7 q pm m1 js4 jv3 pf r15 l1 r17 "
                "es11 es13 es8 t11 C2 x11 b11 t13 C2 t8 x10 x11 Da11 la D b21 C28 l0 P16 dd pos P16 ys15 m0 yv9 ys8 hv5 hs10 hv3 hs9 hs5 z5 z13 z9 zs5",
       "fs": [8, 8, 6, 4]}

f32, bf, i32, u16 = "float32", "bfloat16", "int32", "uint16"
SCRATCH = {k: ("sbuf", [128, c], d) for k, c, d in [
    ("pv", 256, i32), ("sh", 192, i32), ("hd", 8, i32), ("hu", 8, u16),
    ("d0", n, bf), ("d2", n, bf), ("d1", n, bf), ("a1", n + 16, bf), ("mc", n + 16, bf), ("m0", n + 16, bf), ("m2", n + 16, bf),
    ("zer", 32, bf), ("neg", 32, bf), ("pos", 32, bf), ("kk", 32, bf), ("j16", 192, f32), ("idt", 128, f32),
    ("one", 128, bf), ("eyf", 128, f32), ("eyb", 128, bf), ("ts1", n, f32),
    ("pj", 4, i32), ("pm", 4, i32), ("pf", 4, f32),
    ("val", SL, f32), ("z2s", ZW, f32), ("z2v", ZW, f32), ("z3s", ZW, f32), ("z3v", ZW, f32),
    ("z2sw", 128, f32), ("z2vw", 128, f32), ("z3sw", 128, f32), ("z3vw", 128, f32),
    ("ty", 192, i32), ("tz", 192, f32), ("tw", 192, f32),
    ("pu", 256, u16), ("su", 96, u16), ("so", 192, u16), ("l0", 128, u16), ("l1", 128, u16),
    ("f1", W, f32), ("w2", W + SL, f32), ("f0", W + SL, f32), ("u2", n, f32), ("r1", n, f32), ("q1", n, f32), ("c1", n, f32),
    ("p1", n, f32), ("x1", n, f32), ("dall", W // 2 + 8, f32), ("dd", 4, f32)]}
SCRATCH["t1"] = ("psum", [128, n], f32)
SCRATCH["pa"] = ("psum", [128, n], f32)
SEMAPHORES = ["e%d" % k for k in range(100)] + ["arr1", "arr2", "arr3", "arrd", "out1", "out2", "out3", "outd"]


def engine_sets(topo, src, peers, share=1):
    eng = topo.engines(src, peers[0])
    far = [p for p in peers if topo.die(p) != topo.die(src)]
    near = [p for p in peers if topo.die(p) == topo.die(src)]
    res = {}
    for group, pool in ((far, eng[0::2]), (near, eng[1::2])):
        pool = pool[:len(pool) // share]
        size = {p: 1 for p in group}
        grown = True
        while grown:
            grown = False
            for p in sorted(group, key=lambda x: size[x]):
                if sum(size.values()) + size[p] <= len(pool):
                    size[p] *= 2
                    grown = True
                    break
        at = 0
        for p in group:
            res[p] = pool[at:at + size[p]]
            at += size[p]
    return res


def runs(slots):
    out = []
    for s in slots:
        if out and out[-1][1] == s:
            out[-1][1] = s + 1
        else:
            out.append([s, s + 1])
    return out


def rank_program(g, core, T, topo):
    r = T.rank_of(core)
    if r is None:
        return
    cores = list(T.cores)
    others = [p for p in range(NR) if p != r]
    share = CFG.get("share", {"1": 1, "2": 1, "3": 1, "d": 1})
    mine = {k: engine_sets(topo, core, [cores[p] for p in others], s) for k, s in share.items()}
    going = {k: sum(len(e) for e in mine[k].values()) for k in share}
    coming = {k: sum(len(engine_sets(topo, cores[p], [c for c in cores if c != cores[p]], s)[core]) for p in others) for k, s in share.items()}
    if CFG.get("one"):
        going["d"] = len(topo.engines(core, cores[others[0]]))
        coming["d"] = sum(len(topo.engines(cores[p], core)) for p in others)
    V, S, Y = g.vector, g.scalar, g.sync
    Q = {"v": V, "s": S, "y": Y, "g": g, "t": g.tensor}
    ops = []
    COPY = AF.Silu if CFG.get("silu") else AF.Copy
    zer = "kk" if CFG.get("silu") else "zer"

    def op(q, fn, rd, wr, dma=False, sem=None):
        ops.append({"q": q, "fn": fn, "rd": rd, "wr": wr, "inc": 16 if dma else 1, "sem": sem})

    def send(src, dst, k, rd, lands, to=others):
        def fn():
            tr = []
            if k == "d" and CFG.get("one"):
                tr = [RemoteDMATransfer(dst_ids=[DstId(rid=topo.addr(cores[p])[0], pnc=topo.addr(cores[p])[1]) for p in others],
                                        dma_engine_mask=topo.mask(core, cores[others[0]]), remote_sem=T.sem.arrd,
                                        srcs=[src(r)], dsts=[dst(p) for p in others])]
            for p in to if not tr else []:
                rid, pid, _ = topo.addr(cores[p])
                tr.append(RemoteDMATransfer(dst_ids=[DstId(rid=rid, pnc=pid)], dma_engine_mask=sum(1 << e for e in mine[k][cores[p]]),
                                            remote_sem=T.sem["arr" + k], src=src(p), dst=dst(p)))
            g.remote_dma_fused(tr, local_sem=T.sem["out" + k])
            return None
        op("g", fn, rd, [])
        if lands:
            op("x", None, [], lands, sem=("arr" + k, coming[k]))

    def ts(out, a, s1, s2, o0, o1, rd, wr):
        if o1 is None:
            op("v", lambda: V.tensor_scalar(out, a, s1, None, o0), rd, wr)
        else:
            op("v", lambda: V.tensor_scalar(out, a, s1, s2, o0, o1), rd, wr)

    def tt(out, a, b, o, rd, wr):
        op("v", lambda: V.tensor_tensor(out, a, b, o), rd, wr)

    def cp(out, a, rd, wr):
        op("v", lambda: V.tensor_copy(out, a), rd, wr)

    def scan(out, d0, d1, init, o0, o1, rd, wr):
        op("v", lambda: V.tensor_tensor_scan(out, d0, d1, init, o0, o1), rd, wr)

    def act(out, a, func, rd, wr, **kw):
        op("s", lambda: S.activation(out, a, func, **kw), rd, wr)

    def dma(q, out, a, rd, wr):
        op(q, lambda: Q[q].dma_start(out, a), rd, wr, dma=True)

    def fill(name, lo, hi, c):
        op("v", lambda: V.memset(T[name][:, lo:hi], c), [], [(name, lo, hi)])

    def iota(name, lo, hi, step, base, mult):
        if SCRATCH[name][2] == i32:
            op("g", lambda: g.iota(T[name][:, lo:hi], [[step, hi - lo]], base, mult), [], [(name, lo, hi)])
        else:
            op("g", lambda: g.iota(T[name][:, lo:hi], [[step, hi - lo]], base, mult, allow_small_or_imprecise_dtypes=True), [], [(name, lo, hi)])

    def rev(name, lo, hi):
        return T[name][:, hi - 1::-1] if lo == 0 else T[name][:, hi - 1:lo - 1:-1]

    def whole(name):
        return (name, 0, SCRATCH[name][1][1])

    def gather(q, out, olo, win, wlo, whi, off, clo, chi):
        src = T[win][:, wlo:whi].indirect(T[off][:, clo:chi])
        ohi = olo + 16 * (chi - clo)
        if q == "v":
            cp(T[out][:, olo:ohi], src, [(win, wlo, whi), (off, clo, chi)], [(out, olo, ohi)])
        else:
            act(T[out][:, olo:ohi], src, COPY, [(win, wlo, whi), (off, clo, chi)], [(out, olo, ohi)])

    def scatter(q, win, wlo, whi, off, clo, chi, src, slo):
        out, shi = T[win][:, wlo:whi].indirect(T[off][:, clo:chi]), slo + 16 * (chi - clo)
        if q == "v":
            cp(out, T[src][:, slo:shi], [(off, clo, chi), (src, slo, shi)], [(win, wlo, whi)])
        else:
            act(out, T[src][:, slo:shi], AF.Silu, [(off, clo, chi), (src, slo, shi)], [(win, wlo, whi)])

    def mark(name, stage, const):
        scatter("v", name, 0, n, "hu", 2 * stage, 2 * stage + 2, const, 0)

    a_ = lambda name: T[name][:, :]

    def ship_places(lo, hi):
        a = lambda name: T[name][:, lo:hi]
        if CFG.get("pp"):
            z, w = ("t1", lo, hi), ("t1", 256 + lo, 256 + hi)
        else:
            z, w = ("tz", lo, hi), ("tw", lo, hi)
        b = lambda x: T[x[0]][:, x[1]:x[2]]
        return [
            lambda: ts(a("ty"), a("sh"), EMPTY, None, A.bitwise_and, None, [("sh", lo, hi)], [("ty", lo, hi)]),
            lambda: ts(b(z), a("ty"), 2047.0, None, A.mult, None, [("ty", lo, hi)], [z]),
            lambda: tt(b(w), a("sh"), b(z), A.add, [("sh", lo, hi), z], [w]),
            lambda: tt(a("tz"), b(w), a("j16"), A.min, [w, whole("j16")], [("tz", lo, hi)]),
            lambda: ts(a("so"), a("tz"), 0.0625, None, A.mult, None, [("tz", lo, hi)], [("so", lo, hi)])]

    order = CFG["order"].split()
    total = lambda head: sum(int(x[len(head):]) for x in order if x[:len(head)] == head and x[len(head):].isdigit())
    at = {}

    def down(key, k):
        hi = at.get(key, n)
        at[key] = hi - U * k
        return hi - U * k, hi

    def up(key, k):
        lo = at.get(key, 0)
        at[key] = lo + U * k
        return lo, lo + U * k

    def slots(key, k):
        lo = at.get(key, 0)
        at[key] = lo + k
        return [[lo, lo + k]] if cmp else runs(others[lo:lo + k])

    def need(ok):
        assert ok

    m2 = "m2" if "m2" in order else "mc"
    cmp = CFG.get("cmp")
    LS = 84 if cmp else 96
    here = (lambda p: p - (p > r)) if cmp else (lambda p: p)
    there = (lambda p: r - (r > p)) if cmp else (lambda p: r)
    sp2, sp1, spw = ship_places(LS, 2 * LS), ship_places(0, LS), ship_places(0, 2 * LS)
    h = n // 2

    def u2_scan(k):
        lo, hi = down("u", k)
        scan(rev("u2", lo, hi), rev(m2, lo + 1, hi + 1), rev("d2", lo, hi), float(OFF) if hi == n else T.u2[:, hi:hi + 1], A.min, A.add,
             [whole(m2), ("d2", lo, hi)] + ([] if hi == n else [("u2", hi, hi + 1)]), [("u2", lo, hi)])

    def u2_scatter(k):
        lo, hi = down("a", k)
        need(lo >= at["u"] and at.get("f", SL) + U * CFG.get("fg", 0) >= SL)
        scatter("s", "w2", SL, SL + W, "pu", 128 + lo // 16, 128 + hi // 16, "u2", lo)
        if lo == 0:
            send(lambda p: T.w2[:, W + CAP * p:W + CAP * p + CAP], lambda p: T.w2[:, CAP * there(p):CAP * there(p) + CAP], "2", [("w2", W, W + SL)], [("w2", 0, SL)])
            late_constants()

    def c0_scan(k):
        lo, hi = up("c", k)
        scan(T[cw][:, co + lo:co + hi], T.mc[:, lo:hi], T.d0[:, lo:hi], float(OFF) if lo == 0 else T[cw][:, co + lo - 1:co + lo], A.min, A.add,
             [whole("mc"), ("d0", lo, hi)] + ([] if lo == 0 else [(cw, co + lo - 1, co + lo)]), [(cw, co + lo, co + hi)])

    cw, co, sb, so = ("f0", SL, "f1", 0) if "cut" in CFG else ("f1", 0, "f0", W)

    def ship_gather(q, k):
        need(at["c"] == n)
        if CFG.get("two"):
            first = sorted(others, key=lambda p: topo.die(cores[p]) == topo.die(core))
            far = [p for p in others if topo.die(cores[p]) != topo.die(core)]
            lo = at.get("A", 0)
            at["A"] = lo + k
            for a, b in runs(sorted(here(p) for p in first[lo:lo + k])):
                gather(q, sb, so + CAP * a, cw, co, co + n, "su", 12 * a, 12 * b)
            for to, end in ((far, len(far)), (first[len(far):], NR - 1)):
                if lo < end <= lo + k:
                    send(lambda p: T[sb][:, so + CAP * here(p):so + CAP * here(p) + CAP], lambda p: T[cw][:, co + n + CAP * r:co + n + CAP * r + CAP], "1",
                         [(sb, so + CAP * here(p), so + CAP * here(p) + CAP) for p in to], [(cw, co + n, co + W)] if end == NR - 1 else None, to)
            if at["A"] == NR - 1:
                op("x", None, [], [("f0", W, W + SL)], sem=("out1", going["1"]))
                late_constants()
            return
        for a, b in slots("A", k):
            gather(q, sb, so + CAP * a, cw, co, co + n, "su", 12 * a, 12 * b)
        if at["A"] == NR - 1:
            send(lambda p: T[sb][:, so + CAP * here(p):so + CAP * here(p) + CAP], lambda p: T[cw][:, co + n + CAP * r:co + n + CAP * r + CAP], "1",
                 [(sb, so, so + SL)], [(cw, co + n, co + W)])
            if sb == "f0":
                op("x", None, [], [("f0", W, W + SL)], sem=("out1", going["1"]))
            late_constants()

    def late_constants():
        if at.get("A") == NR - 1 and at.get("a") == 0:
            iota("m0", 0, n + 16, 0, 0, 0)

    def ship_inverse(z, lo, key, q, k):
        need(not (sp2 if lo else sp1))
        for a, b in slots(key, k):
            scatter(q, z + q, 0, ZW, "so", lo + 12 * a, lo + 12 * b, "val", CAP * a)
        at[key + q] = at.get(key + q, 0) + k
        if at[key + q] == total(key + q):
            dma("y", a_(z + q + "w"), T[z + q][0:128:16, 0:n], [(z + q, 0, n)], [whole(z + q + "w")])

    def offsets(l, z, key, half=False):
        need(at[key] == NR - 1)
        parts = [z + q + "w" for q in "sv" if total(key + q)]
        if len(parts) == 2 and l + "a" not in at:
            tt(a_(parts[0]), a_(parts[0]), a_(parts[1]), A.min, [whole(parts[0]), whole(parts[1])], [whole(parts[0])])
        if half:
            need(l not in at)
            at[l + "a"] = 1
            return
        ts(a_(l), a_(parts[0]), T.pf[:, 0:1], None, A.subtract, None, [whole(parts[0]), whole("pf")], [whole(l)])
        at[l] = 1

    pe = CFG.get("pe")
    t1, r1, rkey, p1 = ("ts1", "pa", "R", "t1") if pe else ("t1", "r1", "r", "p1")

    def r1_gather(k, q="v"):
        lo, hi = down("r", k)
        need(at["A"] == NR - 1)
        if pe:
            gather(q, "r1", lo, "f1", 0, W, "pu", lo // 16, hi // 16)
        else:
            need(q == "v")
            tt(T.r1[:, lo:hi], T[cw][:, co:co + W].indirect(T.pu[:, lo // 16:hi // 16]), T.d1[:, lo:hi], A.add,
               [(cw, co, co + W), ("pu", 0, 128), whole("d1")], [("r1", lo, hi)])

    def pass_on(out, src, eye, lo, hi, start, stop):
        op("t", lambda: g.tensor.matmul(T[out][:, lo:hi], a_(eye), T[src][:, lo:hi], start, stop), [whole(eye), (src, lo, hi)], [(out, lo, hi)])

    def d1_pe():
        for lo in range(n - 512, -1, -512):
            pass_on("pa", "d1", "eyb", lo, lo + 512, True, False)

    def r1_pe():
        lo, hi = down("R", 8)
        need(lo >= at["r"] and at["dpe"])
        pass_on("pa", "r1", "eyf", lo, hi, False, True)

    def t1_pe():
        lo, hi = down("T", 8)
        need(lo >= at["t"])
        pass_on("t1", "ts1", "eyf", lo, hi, True, False)

    def c1_pe():
        lo, hi = up("P", 8)
        need(hi <= at["C"] and at["T"] == 0)
        pass_on("t1", "c1", "eyf", lo, hi, False, True)

    def eyes():
        fill("one", 0, 128, 1.0)
        for e in ("eyf", "eyb"):
            op("g", lambda e=e: g.affine_select(a_(e), a_("one"), [[-1, 128]], A.is_equal, 0.0, 0, 1), [whole("one")], [whole(e)])

    cut = U * CFG.get("cut", 0)
    fused = "cut" in CFG

    def side(lo, hi):
        need(lo >= cut or hi <= cut)
        return ("t1", "c1") if lo >= cut else ("ts1", "t1")

    def t1_scan_f(k):
        lo, hi = down("t", k)
        need(lo >= at["e"] and at["m1"])
        o, i = side(lo, hi)[0], side(hi, hi + 1)[0]
        scan(rev(o, lo, hi), rev("a1", lo + 1, hi + 1), rev("q1", lo, hi), -BIG if hi == n else T[i][:, hi:hi + 1], A.add, A.max,
             [("q1", lo, hi), whole("a1")] + ([] if hi == n else [(i, hi, hi + 1)]), [(o, lo, hi)])

    def x1_scatter_f(k):
        lo, hi = down("b", k)
        need(at["r"] == 0)
        if side(lo, hi)[0] == "t1":
            need(lo >= at["x"])
            scatter("s", "f0", SL, SL + W, "pu", lo // 16, hi // 16, "x1", lo)
        else:
            need(lo >= at["t"])
            tt(T.f0[:, SL:SL + W].indirect(T.pu[:, lo // 16:hi // 16]), T.ts1[:, lo:hi], T.r1[:, lo:hi], A.add,
               [("ts1", lo, hi), ("r1", lo, hi), ("pu", 0, 128)], [("f0", SL, SL + W)])
        if lo == 0:
            send(lambda p: T.f0[:, W + CAP * p:W + CAP * p + CAP], lambda p: T.f0[:, CAP * r:CAP * r + CAP], "3", [("f0", W, W + SL)], [("f0", 0, SL)])

    def c1_scan_f(k):
        lo, hi = up("C", k)
        need(at["r"] == 0 and at["m1"] and not sp1 and not sp2)
        o, i = side(lo, hi)[1], side(lo - 1, lo)[1]
        scan(T[o][:, lo:hi], T.a1[:, lo:hi], T.r1[:, lo:hi], 0.0 if lo == 0 else T[i][:, lo - 1:lo], A.add, A.max,
             [whole("a1"), whole("r1")] + ([] if lo == 0 else [(i, lo - 1, lo)]), [(o, lo, hi)])

    def p1_add_f(k):
        lo, hi = up("P", k)
        need(hi <= at["C"] and at["t"] == 0)
        a, b = side(lo, hi)
        tt(T.p1[:, lo:hi], T[a][:, lo:hi], T[b][:, lo:hi], A.add, [(a, lo, hi), (b, lo, hi)], [("p1", lo, hi)])

    def own_end_f(name, lo, half):
        need(at["b"] == 0 if name == "f0" else at["P"] == n and "y" not in at)
        at["D"] = half
        scan(T.dall[:, 0:half], T[name][:, lo:lo + half], T[name][:, lo + half:lo + 2 * half], 0.0, A.max, A.max, [(name, lo, lo + 2 * half)], [("dall", 0, half)])
        place = lambda p: half + (r if r < p else r - 1)
        send(lambda p: T.dall[:, half - 1:half], lambda p: T.dall[:, place(p):place(p) + 1], "d", [("dall", 0, half)], [("dall", half, half + 8)])

    def q1_gather(q, k):
        lo, hi = down("e", k)
        need(at["l1"] and at["a"] == 0)
        gather(q, "q1", lo, "w2", 0, W, "l1", lo // 16, hi // 16)

    def t1_scan(k):
        lo, hi = down("t", k)
        need(lo >= at["e"] and at["m1"])
        scan(rev(t1, lo, hi), rev("a1", lo + 1, hi + 1), rev("q1", lo, hi), -BIG if hi == n else T[t1][:, hi:hi + 1], A.add, A.max,
             [("q1", lo, hi), whole("a1")] + ([] if hi == n else [(t1, hi, hi + 1)]), [(t1, lo, hi)])

    def x1_add(k):
        lo, hi = down("x", k)
        need(lo >= at["t"] and lo >= at[rkey])
        tt(T.x1[:, lo:hi], T[r1][:, lo:hi], T[t1][:, lo:hi], A.add, [(r1, lo, hi), (t1, lo, hi)], [("x1", lo, hi)])

    def x1_scatter(k):
        lo, hi = down("b", k)
        need(lo >= at["x"])
        scatter("s", "f0", SL, SL + W, "pu", lo // 16, hi // 16, "x1", lo)
        if lo == 0:
            need(at["D"] and (at.get("last") or not cmp))
            send(lambda p: T.f0[:, W + CAP * p:W + CAP * p + CAP], lambda p: T.f0[:, CAP * there(p):CAP * there(p) + CAP], "3", [("f0", W, W + SL)], [("f0", 0, SL)])

    def own_part(k):
        lo, hi = down("Da", k)
        need(lo >= at["x"] and (lo > 0 or "D" in at))
        a, m = (n - hi) // 2, (lo + hi) // 2
        scan(T.dall[:, a:a + m - lo], T.x1[:, lo:m], T.x1[:, m:hi], 0.0 if a == 0 else T.dall[:, a - 1:a], A.max, A.max,
             [("x1", lo, hi)] + ([("dall", a - 1, a)] if a else []), [("dall", a, a + m - lo)])

    def own_end():
        need(at["x"] == 0)
        at["D"] = h
        own_part(at.get("Da", n) // U)
        place = lambda p: h + (r if r < p else r - 1)
        send(lambda p: T.dall[:, h - 1:h], lambda p: T.dall[:, place(p):place(p) + 1], "d", [("dall", 0, h)], [("dall", h, h + 8)])

    def c1_scan(k):
        lo, hi = up("C", k)
        need(at[rkey] == 0 and at["m1"])
        scan(T.c1[:, lo:hi], T.a1[:, lo:hi], T[r1][:, lo:hi], 0.0 if lo == 0 else T.c1[:, lo - 1:lo], A.add, A.max,
             [whole("a1"), whole(r1)] + ([] if lo == 0 else [("c1", lo - 1, lo)]), [("c1", lo, hi)])

    def p1_add(k):
        lo, hi = up("P", k)
        need(hi <= at["C"] and at["t"] == 0)
        tt(T.p1[:, lo:hi], T.c1[:, lo:hi], T.t1[:, lo:hi], A.add, [("c1", lo, hi), whole("t1")], [("p1", lo, hi)])

    def plan_end():
        need(at["D"])
        at["dd"] = 1
        e = at["D"]
        op("v", lambda: V.tensor_reduce(T.dd[:, 0:1], T.dall[:, e - 1:e + 7], AxisListType.X, A.max), [whole("dall")], [whole("dd")])

    def rest(q, out, src, rd, wr):
        need(at["dd"])
        if q == "s":
            act(out, src, AF.Identity, rd + [whole("dd")], wr, bias=T.dd[:, 0:1], scale=-1.0)
        else:
            ts(out, src, -1.0, T.dd[:, 0:1], A.mult, A.add, rd + [whole("dd")], wr)

    def slack1(q, k):
        lo, hi = up("y", k)
        need(hi <= at["P"])
        rest(q, T.p1[:, lo:hi], T[p1][:, lo:hi], [(p1, lo, hi)], [("p1", lo, hi)])
        if not CFG.get("sep"):
            store1("y", k)

    def store1(q, k):
        lo, hi = up("Y", k)
        need(hi <= at["y"])
        dma(q, T.y[:, n + lo:n + hi], T.p1[:, lo:hi], [("p1", lo, hi)], [("y", n + lo, n + hi)])

    def store0(q, k):
        lo, hi = down("Z", k)
        need(lo >= at["z"])
        dma(q, T.y[:, lo:hi], T.u2[:, lo:hi], [("u2", lo, hi)], [("y", lo, hi)])

    def x0_gather(q, lo, hi):
        need(at["l0"] and at["b"] == 0)
        rest(q, T.q1[:, lo:hi], T.f0[:, 0:W].indirect(T.l0[:, lo // 16:hi // 16]), [("f0", 0, W), whole("l0")], [("q1", lo, hi)])

    def x0_scalar():
        at["gs"] = n - U * total("gv")
        for k in CFG["fs"]:
            x0_gather("s", *down("gs", k))

    def slack0(k, q="y"):
        lo, hi = down("z", k)
        need(at["m0"] and (lo >= at["h"] if "h" in at else at["gs"] == 0 and at["gv"] == n - U * total("gv")))
        scan(rev("u2", lo, hi), rev("m0", lo + 1, hi + 1), rev("q1", lo, hi), BIG if hi == n else T.u2[:, hi:hi + 1], A.max, A.min,
             [whole("m0"), ("q1", lo, hi)] + ([] if hi == n else [("u2", hi, hi + 1)]), [("u2", lo, hi)])
        if not CFG.get("sep"):
            store0(q, k)

    def warm():
        fill("w2", W, W + 256, float(OFF))
        act(T.w2[:, W + 256:W + 512], T.w2[:, W:W + 256], AF.Silu, [("w2", W, W + 256)], [("w2", W + 256, W + 512)])
        act(T.w2[:, W + 512:W + 1024], T.w2[:, W:W + 512], COPY, [("w2", W, W + 512)], [("w2", W + 512, W + 1024)])

    def spare(q, k):
        lo, hi = up("f", k)
        if q == "v":
            fill("w2", W + lo, W + hi, float(OFF))
        elif q == "g":
            iota("w2", W + lo, W + hi, 0, OFF, 0)
        else:
            need(hi - lo <= lo)
            act(T.w2[:, W + lo:W + hi], T.w2[:, W:W + hi - lo], AF.Silu, [("w2", W, W + hi - lo)], [("w2", W + lo, W + hi)])

    def once(key, fn):
        def run():
            at[key] = 1
            fn()
        return run
    plain = {
        "warm": warm, "mc": lambda: fill("mc", 0, n + 16, BIG), "m2": lambda: fill("m2", 0, n + 16, BIG),
        "fill": lambda: fill("w2", W + 1024, W + SL, float(OFF)),
        "fills": lambda: act(T.w2[:, W + 1024:W + SL], T.w2[:, W:W + 512], COPY, [("w2", W, W + 512)], [("w2", W + 1024, W + SL)]),
        "kk": lambda: fill("kk", 0, 32, float(OFF)), "pos": lambda: fill("pos", 0, 32, BIG), "zer": lambda: fill("zer", 0, 32, 0.0),
        "neg": lambda: fill("neg", 0, 32, -BIG),
        "hu": lambda: cp(T.hu[:, 0:6], T.hd[:, 0:6], [whole("hd")], [whole("hu")]),
        "su": lambda: cp(T.su[:, 0:LS], T.sh[:, 0:LS], [("sh", 0, LS)], [whole("su")]),
        "last": once("last", lambda: fill("f0", W + SL - CAP, W + SL, float(OFF))),
        "pu1": lambda: cp(T.pu[:, 0:128], T.pv[:, 0:128], [("pv", 0, 128)], [("pu", 0, 128)]),
        "pu2": lambda: cp(T.pu[:, 128:256], T.pv[:, 128:256], [("pv", 128, 256)], [("pu", 128, 256)]),
        "pu": lambda: cp(a_("pu"), a_("pv"), [whole("pv")], [whole("pu")]),
        "m0z": lambda: mark("mc", 0, zer), "m0b": lambda: mark("mc", 0, "pos"), "m2k": lambda: mark(m2, 2, "kk"), "m2b": lambda: mark("mc", 2, "pos"),
        "m1": once("m1", lambda: mark("a1", 1, "neg")), "m0": once("m0", lambda: mark("m0", 0, "pos")),
        "p": lambda: sp2.pop(0)(), "q": lambda: sp1.pop(0)(),
        "pm": lambda: ts(T.pm[:, 0:1], T.pj[:, 0:1], 112, None, A.bitwise_and, None, [whole("pj")], [whole("pm")]),
        "pf": lambda: ts(T.pf[:, 0:1], T.pm[:, 0:1], OFF - 0.25, None, A.add, None, [whole("pm")], [whole("pf")]),
        "l1": lambda: offsets("l1", "z2", "i"), "l0": lambda: offsets("l0", "z3", "j"),
        "la": lambda: offsets("l0", "z3", "j", True), "lb": lambda: offsets("l1", "z2", "i", True),
        "eye": eyes, "dpe": once("dpe", d1_pe), "R": r1_pe, "T": t1_pe, "P": c1_pe, "w": lambda: (sp1.pop(0), sp2.pop(0), spw.pop(0)()),
        "D": own_end, "dd": plan_end, "gs": x0_scalar}
    counted = {
        "u": u2_scan, "a": u2_scatter, "c": c0_scan, "as": lambda k: ship_gather("s", k), "av": lambda k: ship_gather("v", k),
        "is": lambda k: ship_inverse("z2", LS, "i", "s", k), "iv": lambda k: ship_inverse("z2", LS, "i", "v", k),
        "js": lambda k: ship_inverse("z3", 0, "j", "s", k), "jv": lambda k: ship_inverse("z3", 0, "j", "v", k),
        "r": r1_gather, "rs": lambda k: r1_gather(k, "s"), "es": lambda k: q1_gather("s", k), "ev": lambda k: q1_gather("v", k), "t": t1_scan, "x": x1_add, "b": x1_scatter,
        "C": c1_scan, "P": p1_add, "ys": lambda k: slack1("s", k), "yv": lambda k: slack1("v", k),
        "gv": lambda k: x0_gather("v", *down("gv", k)), "z": slack0,
        "Yy": lambda k: store1("y", k), "Ys": lambda k: store1("s", k), "Yg": lambda k: store1("g", k),
        "Zy": lambda k: store0("y", k), "Zs": lambda k: store0("s", k), "Zg": lambda k: store0("g", k),
        "Da": own_part, "zs": lambda k: slack0(k, "s"), "fv": lambda k: spare("v", k), "fs": lambda k: spare("s", k),
        "hs": lambda k: x0_gather("s", *down("h", k)), "hv": lambda k: x0_gather("v", *down("h", k))}

    if fused:
        counted.update(t=t1_scan_f, b=x1_scatter_f, C=c1_scan_f, P=p1_add_f)
        plain.update(Dw=lambda: own_end_f("f0", SL, W // 2), Dp=lambda: own_end_f("p1", 0, h), own=lambda: fill("f0", W + CAP * r, W + CAP * r + CAP, 0.0))

    if "mc" not in order:
        iota("mc", 0, n + 16, 0, int(BIG), 0)
    if CFG.get("fg"):
        iota("w2", W + SL - U * CFG["fg"], W + SL, 0, OFF, 0)
    iota("pj", 0, 1, 0, 0, 1)
    iota("idt", 0, 128, 16, n, 1)
    if CFG.get("fg") and cmp:
        at["last"] = 1
        iota("f0", W + SL - CAP, W + SL, 0, OFF, 0)
    loads = list(CFG["loads"])
    if "a1" not in [x[1] for x in loads]:
        loads += [("y", z, 0, n) for z in ("z2s", "z2v", "z3s", "z3v", "d1")] + [("y", "a1", 0, n + 16)]
    for q, name, lo, hi in loads:
        if name[0] == "z":
            if total({"z2": "i", "z3": "j"}[name[:2]] + name[2]):
                dma(q, T[name][0:128:16, 0:n], a_("idt"), [whole("idt")], [(name, 0, n)])
            continue
        if name == "sh" and cmp:
            to = 0
            for a, b in ((0, 12 * r), (12 * r + 12, 96 + 12 * r), (108 + 12 * r, 192)):
                if b > a:
                    dma(q, T.sh[:, to:to + b - a], T.ship[:, a:b], [], [("sh", to, to + b - a)])
                to += b - a
            continue
        src, base = {"hd": (T.heads, 0), "pv": (T.prev, 0), "sh": (T.ship, 0), "d0": (T.dur, 0), "d2": (T.dur, 2 * n), "d1": (T.dur, n), "a1": (T.dur, n)}[name]
        dma(q, T[name][:, lo:hi], src[:, base + lo:base + hi], [], [(name, lo, hi)])
    op("g", lambda: g.iota(T.j16[:, 0:2 * LS], [[0, 2], [256, LS]], 16 * n, 16, allow_small_or_imprecise_dtypes=True), [], [whole("j16")])
    for lo, hi in ([(0, SL - CAP)] if cmp else [(0, 4 * CAP), (4 * CAP, SL)] if CFG.get("val2") else [(0, SL)]):
        iota("val", lo, hi, 1, OFF + lo, 1)
    for x in order:
        if x in plain:
            plain[x]()
        else:
            head = x.rstrip("0123456789")
            counted[head](int(x[len(head):]))
    need(at["Z"] == 0 and at["Y"] == n)
    op("y", None, [("y", 0, 2 * n)], [])

    def meet(a, b):
        return any(x[0] == z[0] and x[1] < z[2] and z[1] < x[2] for x in a for z in b)
    for o in ops:
        o["bank"] = [(x[0], x[1] // 512 * 512, (x[2] + 511) // 512 * 512) for x in o["rd"] + o["wr"] if x[0] in ("t1", "pa")]
    known = {q: set() for q in "vsygxt"}
    closure, waits, used = [], [], set()
    for k, o in enumerate(ops):
        deps = [j for j in range(k) if meet(ops[j]["wr"], o["rd"] + o["wr"]) or meet(ops[j]["rd"], o["wr"])
                or (ops[j]["q"] != o["q"] and meet(ops[j]["bank"], o["bank"]))]
        if o["q"] == "x":
            deps = []
        deps = [j for j in deps if ops[j]["q"] != "g" or ops[j]["wr"]]
        if CFG.get("free") and o["inc"] == 1 and o["q"] in "vs":
            deps = [j for j in deps if ops[j]["q"] != o["q"] or ops[j]["inc"] != 1 or meet(ops[j]["wr"], o["rd"])]
        kn, w = known[o["q"]], []
        for j in sorted(deps, reverse=True):
            if j not in kn:
                w.append(j)
                kn |= closure[j]
        waits.append(w)
        used |= set(w)
        closure.append((set() if o["q"] == "x" else set(kn)) | {k})
    sems, lines = {}, []
    for j in sorted(used):
        if ops[j]["sem"]:
            sems[j] = (T.sem[ops[j]["sem"][0]], ops[j]["sem"][1])
            continue
        kind = (ops[j]["q"], ops[j]["inc"])
        line = next((x for x in lines if x[0] == kind and x[1] in closure[j]), None)
        if line is None:
            line = [kind, j, 0, T.sem["e%d" % len(lines)]]
            lines.append(line)
        line[1], line[2] = j, line[2] + ops[j]["inc"]
        sems[j] = (line[3], line[2])
    for k, o in enumerate(ops):
        for j in reversed(waits[k]):
            Q[o["q"]].wait_ge(sems[j][0], sems[j][1])
        if o["fn"] is not None:
            ins = o["fn"]()
            if k in sems:
                ins.then_inc(sems[k][0], o["inc"])
    for k in share:
        g.wait_ge(T.sem["out" + k], going[k])
